import numpy as np
import ml_dtypes


def mxq(x, axis, fmt="e4m3"):
    dtype, down = {"e4m3": (ml_dtypes.float8_e4m3fn, 7), "e5m2": (ml_dtypes.float8_e5m2, 14)}[fmt]
    v = np.moveaxis(np.asarray(x, np.float32).astype(ml_dtypes.bfloat16).astype(np.float64), axis, -1)
    blocks = v.reshape(v.shape[:-1] + (-1, 32))
    amax = np.abs(blocks).max(-1, keepdims=True)
    byte = np.maximum(np.where(amax > 0, np.frexp(amax)[1] - 1 + 127, 0) - down, 1)
    scale = np.exp2(byte - 127.0)
    codes = (blocks / scale).astype(np.float32).astype(dtype).astype(np.float64)
    return np.moveaxis((codes * scale).reshape(v.shape), -1, axis)


WIDE = False


def mx_kscale(k):
    if not WIDE:
        return np.ones(k)
    levels = np.array([10, -10, 5, -5, 0])
    if k % 512:
        return np.exp2(np.random.permutation(np.resize(levels, k // 32))).repeat(32)
    a = np.empty((k // 512, 16))
    for p in range(k // 512):
        a[p, :8] = np.random.permutation(np.resize(levels, 8))
        for g in range(8):
            far = levels[np.abs(levels - a[p, g]) >= 10]
            a[p, g + 8] = far[np.random.randint(len(far))]
    return np.exp2(a.ravel()).repeat(32)


BF16 = ml_dtypes.bfloat16


def bf(x):
    return np.asarray(x, np.float32).astype(BF16)


def f64(x):
    return np.asarray(x).astype(np.float64)


B, S, D = 4, 1024, 512
TWO = 2


def softmax_last(logit):
    top = np.max(logit, axis=-1, keepdims=True)
    e = np.exp(logit - top)
    return e / np.sum(e, axis=-1, keepdims=True)


def draw0():
    s, t = mx_kscale(D), mx_kscale(S)
    x = bf(np.random.standard_normal((B, S, D)) * s)
    w = bf(np.random.standard_normal((D, S)) * (2.0 / np.sqrt(D)) / s[:, None])
    rnd = bf(np.random.standard_normal((S, S)) * 1.5)
    mix = bf(np.random.uniform(0.5, 0.9, (TWO,)))
    wv = bf(np.random.standard_normal((D, D)) / np.sqrt(D) / s[:, None])
    c = bf(np.random.standard_normal(S) * (0.25 * np.sqrt(S)) * t)
    u = bf((1.0 + 0.1 * np.random.standard_normal(S)) / t)
    return {"x": x, "w": w, "rnd": rnd, "mix": mix, "wv": wv, "c": c, "u": u}


def core(x, w, rnd, mix, wv, c, u):
    mix = f64(mix)
    xq = mxq(f64(x), 2, "e4m3")
    syn = xq @ mxq(f64(w), 0, "e4m3")
    logit = mix[0] * syn + mix[1] * f64(rnd)[None, :, :]
    p = softmax_last(logit)
    pc = p * f64(c)[None, None, :]
    v = f64(u)[None, :, None] * (xq @ mxq(f64(wv), 0, "e4m3"))
    return mxq(pc, 2, "e4m3") @ mxq(v, 1, "e4m3")


def e4m3fn_bytes(y):
    return np.clip(np.asarray(y, np.float64), -448.0, 448.0).astype(np.float32).astype(ml_dtypes.float8_e4m3fn).view(np.uint8)


def e4m3fn_values(b):
    return np.asarray(b, np.uint8).view(ml_dtypes.float8_e4m3fn).astype(np.float64)


def setup_inputs():
    d = draw0()
    x0 = np.asarray(d['x']).astype(np.float64)
    s = (np.max(np.abs(x0), axis=(0, 1), keepdims=True) / 448.0).astype(np.float32)
    out = {}
    for k, v in d.items():
        if k == 'x':
            out['x_bytes'] = e4m3fn_bytes(x0 / s.astype(np.float64))
            out['x_scale'] = s
        else:
            out[k] = v
    return out


def reference(x_bytes, x_scale, w, rnd, mix, wv, c, u):
    return core(e4m3fn_values(x_bytes) * x_scale.astype(np.float64), w, rnd, mix, wv, c, u)

@@ -1,0 +1,377 @@
+from contextlib import ExitStack
+
+import concourse.mybir as mybir
+from concourse.masks import make_identity
+
+B, S, D = 4, 1024, 512
+P = 128
+PACK = 4
+H = S // (P * PACK)
+TILES = S // P
+N_STEPS = B * TILES
+
+F32 = mybir.dt.float32
+BF16 = mybir.dt.bfloat16
+U32 = mybir.dt.uint32
+U8 = mybir.dt.uint8
+FP8 = mybir.dt.float8_e4m3fn
+FP8X4 = mybir.dt.float8_e4m3fn_x4
+Alu = mybir.AluOpType
+Act = mybir.ActivationFunctionType
+AX = mybir.AxisListType
+
+FLOPS = 2 * B * S * D * S + 2 * B * S * D * D + 2 * B * S * S * D
+
+VECTOR_TILES = (N_STEPS - 1,)
+
+
+def tile_mixturedenserandomsynthesizer_t_kernel(tc, x_bytes, x_scale, w, rnd, mix, wv, c, u, out):
+    nc = tc.nc
+    with ExitStack() as ctx:
+        keep = ctx.enter_context(tc.tile_pool(name="keep", bufs=1))
+        work = ctx.enter_context(tc.tile_pool(name="work", bufs=2))
+        ps_syn = ctx.enter_context(tc.psum_pool(name="ps_syn", bufs=2))
+        ps_tr = ctx.enter_context(tc.psum_pool(name="ps_tr", bufs=2))
+        ps_acc = ctx.enter_context(tc.psum_pool(name="ps_acc", bufs=2))
+
+        xs = keep.tile([P, 2 * D], F32, name="xs")
+        nc.scalar.dma_start(out=xs[:, 0:D], in_=x_scale.rearrange("a b k -> (a b k)").partition_broadcast(P))
+        mix_b = keep.tile([P, 2], BF16, name="mix_b")
+        nc.scalar.dma_start(out=mix_b[:], in_=mix.partition_broadcast(P))
+        u_b = keep.tile([P, H, PACK], BF16, name="u_b")
+        nc.scalar.dma_start(out=u_b[:], in_=u.rearrange("(h p t) -> p h t", p=P, t=PACK))
+        c_b = keep.tile([P, S], BF16, name="c_b")
+        nc.scalar.dma_start(out=c_b[:], in_=c.partition_broadcast(P))
+
+        xb = []
+        for b in range(B):
+            xb.append(keep.tile([P, H, PACK, D], U8, name="xb%d" % b, align_bytes=64))
+        xv = x_bytes.rearrange("b (h m t) k -> b m h t k", m=P, t=PACK)
+        w_raw = keep.tile([P, PACK, S], BF16, name="w_raw")
+        wv_raw = keep.tile([P, PACK, D], BF16, name="wv_raw")
+        rnd_raw = keep.tile([P, TILES, S], BF16, name="rnd_raw")
+        rnd_v = rnd.rearrange("(h m t) k -> m h t k", m=P, t=PACK)
+        w_v = w.rearrange("(p j) n -> p j n", j=PACK)
+
+        nc.sync.dma_start(out=xb[0][:, 0], in_=xv[0, :, 0])
+        for n in range(2):
+            nc.sync.dma_start(out=w_raw[:, :, n * 512 : (n + 1) * 512], in_=w_v[:, :, n * 512 : (n + 1) * 512])
+        nc.sync.dma_start(out=rnd_raw[:, 0:2], in_=rnd_v[:, 0, 0:2])
+        nc.sync.dma_start(out=xb[0][:, 1], in_=xv[0, :, 1])
+        nc.sync.dma_start(out=wv_raw[:], in_=wv.rearrange("(p j) n -> p j n", j=PACK))
+        nc.sync.dma_start(out=rnd_raw[:, 2:4], in_=rnd_v[:, 0, 2:4])
+        nc.sync.dma_start(out=rnd_raw[:, 4:8], in_=rnd_v[:, 1])
+        for b in range(1, B):
+            nc.sync.dma_start(out=xb[b][:], in_=xv[b])
+
+        ident = keep.tile([P, P], F32, name="ident")
+        make_identity(nc, ident[:])
+        warm = keep.tile([P, 1], F32, name="warm")
+        nc.vector.memset(warm[:], 0.0)
+        nc.scalar.activation(out=warm[:], in_=warm[:], func=Act.Exp)
+        mix_f = keep.tile([P, 2], F32, name="mix_f")
+        nc.vector.tensor_copy(out=mix_f[:], in_=mix_b[:])
+        u_f = keep.tile([P, H, PACK], F32, name="u_f")
+        nc.vector.tensor_copy(out=u_f[:], in_=u_b[:])
+        c_f = keep.tile([P, S], F32, name="c_f")
+        rnd_f = keep.tile([P, TILES, S], F32, name="rnd_f")
+
+        w_codes = keep.tile([P, S], U32, name="w_codes", align_bytes=64)
+        w_scales = keep.tile([P, S], U8, name="w_scales", align_bytes=64)
+        wv_codes = keep.tile([P, D], U32, name="wv_codes", align_bytes=64)
+        wv_scales = keep.tile([P, D], U8, name="wv_scales", align_bytes=64)
+        x_codes, x_scales, v_codes, v_scales = [], [], [], []
+        for b in range(B):
+            x_codes.append(keep.tile([P, S], U32, name="x_codes%d" % b, align_bytes=64))
+            x_scales.append(keep.tile([P, S], U8, name="x_scales%d" % b, align_bytes=64))
+            v_codes.append(keep.tile([P, H, D], U32, name="v_codes%d" % b, align_bytes=64))
+            v_scales.append(keep.tile([P, H, D], U8, name="v_scales%d" % b, align_bytes=64))
+
+        out_v = out.rearrange("b (h m t) d -> b m h t d", m=P, t=PACK)
+
+        def rnd_scale(i):
+            nc.gpsimd.tensor_scalar(
+                out=rnd_f[:, i], in0=rnd_raw[:, i], scalar1=mix_f[:, 1:2], scalar2=0.0, op0=Alu.mult, op1=Alu.add
+            )
+
+        def weight_copy(raw, width, cols, grouped, on_vector):
+            src = raw[:, :, cols].rearrange("p j n -> p n j")
+            if on_vector:
+                nc.vector.tensor_copy(out=grouped[:], in_=src)
+            else:
+                nc.scalar.copy(out=grouped[:], in_=src)
+
+        def weight_quantize(grouped, codes, scales, cols):
+            nc.vector.quantize_mx(
+                out=codes[:, cols].bitcast(FP8X4),
+                scales=scales[:, cols],
+                in_=grouped[:].rearrange("p n j -> p (n j)"),
+            )
+
+        x_state = {}
+
+        def x_first(b, k):
+            h, t = k // 2, 2 * (k % 2)
+            xw = work.tile([P, 2 * D], BF16, name="xw")
+            nc.vector.tensor_tensor(
+                out=xw[:],
+                in0=xb[b][:, h, t : t + 2, :].rearrange("p t k -> p (t k)").bitcast(FP8),
+                in1=xs[:],
+                op=Alu.mult,
+            )
+            x_state[(b, k)] = xw
+
+        def x_turn(b, k):
+            words = x_state.get((b, k))[:].bitcast(F32)
+            tr = ps_tr.tile([P, 2, 2, P], F32, name="tr")
+            for j in range(2):
+                for e in range(2):
+                    nc.tensor.transpose(tr[:, j, e, :], words[:, 256 * j + e : 256 * (j + 1) : 2], ident[:])
+            x_state[(b, k)] = tr
+
+        def x_second(b, k):
+            tr = x_state.get((b, k))
+            xg = work.tile([P, 2, P, PACK], BF16, name="xg", align_bytes=64)
+            nc.scalar.copy(out=xg[:].bitcast(F32), in_=tr[:].rearrange("p j e q -> p j q e"))
+            x_state[(b, k)] = xg
+
+        def x_third(b, k):
+            xg = x_state.get((b, k))
+            cols = slice(256 * k, 256 * (k + 1))
+            nc.vector.quantize_mx(
+                out=x_codes[b][:, cols].bitcast(FP8X4),
+                scales=x_scales[b][:, cols],
+                in_=xg[:].rearrange("p j q t -> p (j q t)"),
+            )
+
+        v_state = {}
+
+        def v_bank(b, h, dj):
+            if dj == 0:
+                v_state[(b, h)] = work.tile([P, D, PACK], BF16, name="vg", align_bytes=64)
+            vg = v_state.get((b, h))
+            acc = ps_acc.tile([P, PACK, P], F32, name="acc")
+            d_cols = slice(dj * P, (dj + 1) * P)
+            for t in range(PACK):
+                r_cols = slice((h * PACK + t) * P, (h * PACK + t + 1) * P)
+                nc.tensor.matmul_mx(
+                    out=acc[:, t, :],
+                    lhsT=x_codes[b][:, r_cols].bitcast(FP8X4),
+                    lhsT_scale=x_scales[b][:, r_cols],
+                    rhs=wv_codes[:, d_cols].bitcast(FP8X4),
+                    rhs_scale=wv_scales[:, d_cols],
+                    start=True,
+                    stop=True,
+                )
+            nc.vector.tensor_tensor(
+                out=vg[:, d_cols, :],
+                in0=acc[:].rearrange("p t d -> p d t"),
+                in1=u_f[:, h : h + 1, :].to_broadcast([P, P, PACK]),
+                op=Alu.mult,
+            )
+
+        def v_quantize(b, h):
+            vg = v_state.get((b, h))
+            nc.vector.quantize_mx(
+                out=v_codes[b][:, h, :].bitcast(FP8X4),
+                scales=v_scales[b][:, h, :],
+                in_=vg[:].rearrange("p d t -> p (d t)"),
+            )
+
+        st = {}
+
+        def syn(i):
+            b, r = i // TILES, i % TILES
+            ps = ps_syn.tile([P, 2, 512], F32, name="ps")
+            cols = slice(r * P, (r + 1) * P)
+            for n in range(2):
+                keys = slice(n * 512, (n + 1) * 512)
+                nc.tensor.matmul_mx(
+                    out=ps[:, n, :],
+                    lhsT=x_codes[b][:, cols].bitcast(FP8X4),
+                    lhsT_scale=x_scales[b][:, cols],
+                    rhs=w_codes[:, keys].bitcast(FP8X4),
+                    rhs_scale=w_scales[:, keys],
+                    start=True,
+                    stop=True,
+                )
+            st[("ps", i)] = ps
+
+        def mix_max(i):
+            r = i % TILES
+            ps = st.get(("ps", i))
+            logit = work.tile([P, S], F32, name="logit", bufs=3)
+            for n in range(2):
+                keys = slice(n * 512, (n + 1) * 512)
+                nc.vector.scalar_tensor_tensor(
+                    out=logit[:, keys],
+                    in0=ps[:, n, :],
+                    scalar=mix_f[:, 0:1],
+                    in1=rnd_f[:, r, keys],
+                    op0=Alu.mult,
+                    op1=Alu.add,
+                )
+            nmax = work.tile([P, 1], F32, name="nmax", bufs=4)
+            nc.vector.tensor_reduce(out=nmax[:], in_=logit[:], axis=AX.X, op=Alu.max, negate=True)
+            st[("logit", i)] = (logit, nmax)
+
+        def exponent(i):
+            logit, nmax = st.get(("logit", i))
+            e = work.tile([P, S], F32, name="e", bufs=3)
+            total = work.tile([P, 1], F32, name="total", bufs=4)
+            nc.scalar.activation(out=e[:], in_=logit[:], func=Act.Exp, bias=nmax[:], accum_out=total[:])
+            st[("e", i)] = (e, total)
+
+        def invert(i):
+            total = st.get(("e", i))[1]
+            rinv = work.tile([P, 1], F32, name="rinv", bufs=4)
+            nc.vector.reciprocal(out=rinv[:], in_=total[:])
+            st[("rinv", i)] = rinv
+
+        def gain(i):
+            e = st.get(("e", i))[0]
+            if i in VECTOR_TILES:
+                return
+            ec = work.tile([P, S], F32, name="ec", bufs=3)
+            nc.gpsimd.tensor_tensor(out=ec[:], in0=e[:], in1=c_f[:], op=Alu.mult)
+            st[("ec", i)] = ec
+
+        def normalise(i):
+            rinv = st.get(("rinv", i))
+            pc = work.tile([P, S], BF16, name="pc")
+            if i in VECTOR_TILES:
+                e = st.get(("e", i))[0]
+                nc.vector.scalar_tensor_tensor(out=pc[:], in0=e[:], scalar=rinv[:], in1=c_f[:], op0=Alu.mult, op1=Alu.mult)
+            else:
+                nc.scalar.activation(out=pc[:], in_=st.get(("ec", i))[:], func=Act.Copy, scale=rinv[:])
+            st[("pc", i)] = pc
+
+        def turn(i):
+            pc = st.get(("pc", i))
+            words = pc[:].bitcast(F32)
+            tr = ps_tr.tile([P, 2, 2, P], F32, name="tr")
+            for g in range(2):
+                for e in range(2):
+                    nc.tensor.transpose(tr[:, g, e, :], words[:, 256 * g + e : 256 * (g + 1) : 2], ident[:])
+            st[("tr", i)] = tr
+
+        def turn_out(i):
+            tr = st.get(("tr", i))
+            pg = work.tile([P, 2, P, PACK], BF16, name="pg", bufs=3, align_bytes=64)
+            nc.scalar.copy(out=pg[:].bitcast(F32), in_=tr[:].rearrange("p g e q -> p g q e"))
+            st[("pg", i)] = pg
+
+        def p_quantize(i):
+            pg = st.get(("pg", i))
+            p_codes = work.tile([P, 2, P], U32, name="p_codes", bufs=4, align_bytes=64)
+            p_scales = work.tile([P, 2, P], U8, name="p_scales", bufs=4, align_bytes=64)
+            nc.vector.quantize_mx(
+                out=p_codes[:].rearrange("p g q -> p (g q)").bitcast(FP8X4),
+                scales=p_scales[:].rearrange("p g q -> p (g q)"),
+                in_=pg[:].rearrange("p g q t -> p (g q t)"),
+            )
+            st[("p", i)] = (p_codes, p_scales)
+
+        def product(i):
+            b = i // TILES
+            p_codes, p_scales = st.get(("p", i))
+            acc = ps_acc.tile([P, D], F32, name="acc")
+            for g in range(2):
+                nc.tensor.matmul_mx(
+                    out=acc[:],
+                    lhsT=p_codes[:, g, :].bitcast(FP8X4),
+                    lhsT_scale=p_scales[:, g, :],
+                    rhs=v_codes[b][:, g, :].bitcast(FP8X4),
+                    rhs_scale=v_scales[b][:, g, :],
+                    start=(g == 0),
+                    stop=(g == 1),
+                )
+            st[("acc", i)] = acc
+
+        def store(i):
+            b, r = i // TILES, i % TILES
+            o = work.tile([P, D], F32, name="o", bufs=4)
+            nc.scalar.copy(out=o[:], in_=st.get(("acc", i))[:])
+            nc.sync.dma_start(out=out_v[b, :, r // PACK, r % PACK], in_=o[:])
+
+        plan = {}
+        late = {}
+
+        def put(step, fn, *args):
+            plan.setdefault(step, []).append((fn, args))
+
+        for b in range(B):
+            if b > 0:
+                for k in range(4):
+                    put(8 * b - 2 + k, x_third, b, k)
+                    late.setdefault(8 * b - 4 + k, []).append((x_turn, (b, k)))
+                    late.setdefault(8 * b - 3 + k, []).insert(0, (x_second, (b, k)))
+                    put(8 * b - 4 + k, x_first, b, k)
+            put(8 * b + 2, v_quantize, b, 0)
+            put(8 * b + 4, v_quantize, b, 1)
+            for i in range(8):
+                put(8 * b + i // 2, v_bank, b, i // 4, i % 4)
+        for i in range(2, TILES):
+            put(i - 2, rnd_scale, i)
+
+        with tc.manual_schedule():
+            nc.vector.tensor_copy(out=xs[:, D : 2 * D], in_=xs[:, 0:D])
+            rnd_scale(0)
+            rnd_scale(1)
+            nc.gpsimd.tensor_scalar(out=c_f[:], in0=c_b[:], scalar1=1.0, scalar2=0.0, op0=Alu.mult, op1=Alu.add)
+            w_grouped = []
+            for n in range(2):
+                w_grouped.append(keep.tile([P, 512, PACK], BF16, name="w_grouped%d" % n, align_bytes=64))
+            wv_grouped = keep.tile([P, D, PACK], BF16, name="wv_grouped", align_bytes=64)
+            x_first(0, 0)
+            x_turn(0, 0)
+            x_first(0, 1)
+            x_turn(0, 1)
+            weight_copy(w_raw, 512, slice(0, 512), w_grouped[0], True)
+            x_second(0, 0)
+            x_second(0, 1)
+            weight_copy(w_raw, 512, slice(512, 1024), w_grouped[1], False)
+            x_third(0, 0)
+            x_first(0, 2)
+            x_turn(0, 2)
+            x_third(0, 1)
+            x_second(0, 2)
+            x_first(0, 3)
+            x_turn(0, 3)
+            x_second(0, 3)
+            weight_quantize(w_grouped[0], w_codes, w_scales, slice(0, 512))
+            weight_quantize(w_grouped[1], w_codes, w_scales, slice(512, 1024))
+            x_third(0, 2)
+            x_third(0, 3)
+            weight_copy(wv_raw, D, slice(0, D), wv_grouped, False)
+            syn(0)
+            mix_max(0)
+            weight_quantize(wv_grouped, wv_codes, wv_scales, slice(0, D))
+
+            for s in range(N_STEPS + 5):
+                if 1 <= s <= N_STEPS:
+                    exponent(s - 1)
+                    gain(s - 1)
+                if s + 1 < N_STEPS and s > 0:
+                    syn(s + 1)
+                if s == 0:
+                    syn(1)
+                if 0 <= s - 2 < N_STEPS:
+                    invert(s - 2)
+                    normalise(s - 2)
+                if 0 <= s - 4 < N_STEPS:
+                    p_quantize(s - 4)
+                for fn, args in plan.get(s, []):
+                    fn(*args)
+                if 0 <= s - 4 < N_STEPS:
+                    product(s - 4)
+                if 0 <= s - 2 < N_STEPS:
+                    turn(s - 2)
+                if 0 <= s - 3 < N_STEPS:
+                    turn_out(s - 3)
+                if 0 <= s - 4 < N_STEPS:
+                    store(s - 4)
+                for fn, args in late.get(s, []):
+                    fn(*args)
+                if 0 < s < N_STEPS:
+                    mix_max(s)

@@ -22,7 +22,9 @@ AX = mybir.AxisListType
 
 FLOPS = 2 * B * S * D * S + 2 * B * S * D * D + 2 * B * S * S * D
 
-VECTOR_TILES = (N_STEPS - 1,)
+VECTOR_TILES = (N_STEPS - 3, N_STEPS - 2, N_STEPS - 1)
+GPSIMD_NORM = ()
+GPSIMD_MIX = ()
 
 
 def tile_mixturedenserandomsynthesizer_t_kernel(tc, x_bytes, x_scale, w, rnd, mix, wv, c, u, out):
@@ -30,9 +32,10 @@ def tile_mixturedenserandomsynthesizer_t_kernel(tc, x_bytes, x_scale, w, rnd, mi
     with ExitStack() as ctx:
         keep = ctx.enter_context(tc.tile_pool(name="keep", bufs=1))
         work = ctx.enter_context(tc.tile_pool(name="work", bufs=2))
-        ps_syn = ctx.enter_context(tc.psum_pool(name="ps_syn", bufs=2))
+        ps_syn = ctx.enter_context(tc.psum_pool(name="ps_syn", bufs=3))
         ps_tr = ctx.enter_context(tc.psum_pool(name="ps_tr", bufs=2))
-        ps_acc = ctx.enter_context(tc.psum_pool(name="ps_acc", bufs=2))
+        ps_acc = ctx.enter_context(tc.psum_pool(name="ps_acc", bufs=1))
+        ps_prep = ctx.enter_context(tc.psum_pool(name="ps_prep", bufs=2))
 
         xs = keep.tile([P, 2 * D], F32, name="xs")
         nc.scalar.dma_start(out=xs[:, 0:D], in_=x_scale.rearrange("a b k -> (a b k)").partition_broadcast(P))
@@ -53,11 +56,11 @@ def tile_mixturedenserandomsynthesizer_t_kernel(tc, x_bytes, x_scale, w, rnd, mi
         rnd_v = rnd.rearrange("(h m t) k -> m h t k", m=P, t=PACK)
         w_v = w.rearrange("(p j) n -> p j n", j=PACK)
 
+        nc.sync.dma_start(out=w_raw[:, :, 0:512], in_=w_v[:, :, 0:512])
         nc.sync.dma_start(out=xb[0][:, 0], in_=xv[0, :, 0])
-        for n in range(2):
-            nc.sync.dma_start(out=w_raw[:, :, n * 512 : (n + 1) * 512], in_=w_v[:, :, n * 512 : (n + 1) * 512])
-        nc.sync.dma_start(out=rnd_raw[:, 0:2], in_=rnd_v[:, 0, 0:2])
+        nc.sync.dma_start(out=w_raw[:, :, 512:1024], in_=w_v[:, :, 512:1024])
         nc.sync.dma_start(out=xb[0][:, 1], in_=xv[0, :, 1])
+        nc.sync.dma_start(out=rnd_raw[:, 0:2], in_=rnd_v[:, 0, 0:2])
         nc.sync.dma_start(out=wv_raw[:], in_=wv.rearrange("(p j) n -> p j n", j=PACK))
         nc.sync.dma_start(out=rnd_raw[:, 2:4], in_=rnd_v[:, 0, 2:4])
         nc.sync.dma_start(out=rnd_raw[:, 4:8], in_=rnd_v[:, 1])
@@ -70,9 +73,7 @@ def tile_mixturedenserandomsynthesizer_t_kernel(tc, x_bytes, x_scale, w, rnd, mi
         nc.vector.memset(warm[:], 0.0)
         nc.scalar.activation(out=warm[:], in_=warm[:], func=Act.Exp)
         mix_f = keep.tile([P, 2], F32, name="mix_f")
-        nc.vector.tensor_copy(out=mix_f[:], in_=mix_b[:])
         u_f = keep.tile([P, H, PACK], F32, name="u_f")
-        nc.vector.tensor_copy(out=u_f[:], in_=u_b[:])
         c_f = keep.tile([P, S], F32, name="c_f")
         rnd_f = keep.tile([P, TILES, S], F32, name="rnd_f")
 
@@ -90,9 +91,7 @@ def tile_mixturedenserandomsynthesizer_t_kernel(tc, x_bytes, x_scale, w, rnd, mi
         out_v = out.rearrange("b (h m t) d -> b m h t d", m=P, t=PACK)
 
         def rnd_scale(i):
-            nc.gpsimd.tensor_scalar(
-                out=rnd_f[:, i], in0=rnd_raw[:, i], scalar1=mix_f[:, 1:2], scalar2=0.0, op0=Alu.mult, op1=Alu.add
-            )
+            nc.scalar.activation(out=rnd_f[:, i], in_=rnd_raw[:, i], func=Act.Copy, scale=mix_f[:, 1:2])
 
         def weight_copy(raw, width, cols, grouped, on_vector):
             src = raw[:, :, cols].rearrange("p j n -> p n j")
@@ -123,7 +122,7 @@ def tile_mixturedenserandomsynthesizer_t_kernel(tc, x_bytes, x_scale, w, rnd, mi
 
         def x_turn(b, k):
             words = x_state.get((b, k))[:].bitcast(F32)
-            tr = ps_tr.tile([P, 2, 2, P], F32, name="tr")
+            tr = ps_prep.tile([P, 2, 2, P], F32, name="prep")
             for j in range(2):
                 for e in range(2):
                     nc.tensor.transpose(tr[:, j, e, :], words[:, 256 * j + e : 256 * (j + 1) : 2], ident[:])
@@ -146,11 +145,8 @@ def tile_mixturedenserandomsynthesizer_t_kernel(tc, x_bytes, x_scale, w, rnd, mi
 
         v_state = {}
 
-        def v_bank(b, h, dj):
-            if dj == 0:
-                v_state[(b, h)] = work.tile([P, D, PACK], BF16, name="vg", align_bytes=64)
-            vg = v_state.get((b, h))
-            acc = ps_acc.tile([P, PACK, P], F32, name="acc")
+        def v_product(b, h, dj):
+            acc = ps_prep.tile([P, PACK, P], F32, name="prep")
             d_cols = slice(dj * P, (dj + 1) * P)
             for t in range(PACK):
                 r_cols = slice((h * PACK + t) * P, (h * PACK + t + 1) * P)
@@ -163,6 +159,14 @@ def tile_mixturedenserandomsynthesizer_t_kernel(tc, x_bytes, x_scale, w, rnd, mi
                     start=True,
                     stop=True,
                 )
+            v_state[(b, h, dj)] = acc
+
+        def v_gain(b, h, dj):
+            if dj == 0:
+                v_state[(b, h)] = work.tile([P, D, PACK], BF16, name="vg", align_bytes=64)
+            vg = v_state.get((b, h))
+            acc = v_state.get((b, h, dj))
+            d_cols = slice(dj * P, (dj + 1) * P)
             nc.vector.tensor_tensor(
                 out=vg[:, d_cols, :],
                 in0=acc[:].rearrange("p t d -> p d t"),
@@ -182,12 +186,14 @@ def tile_mixturedenserandomsynthesizer_t_kernel(tc, x_bytes, x_scale, w, rnd, mi
 
         def syn(i):
             b, r = i // TILES, i % TILES
-            ps = ps_syn.tile([P, 2, 512], F32, name="ps")
             cols = slice(r * P, (r + 1) * P)
+            halves = []
             for n in range(2):
+                ps = ps_syn.tile([P, 512], F32, name="ps")
+                halves.append(ps)
                 keys = slice(n * 512, (n + 1) * 512)
                 nc.tensor.matmul_mx(
-                    out=ps[:, n, :],
+                    out=ps[:],
                     lhsT=x_codes[b][:, cols].bitcast(FP8X4),
                     lhsT_scale=x_scales[b][:, cols],
                     rhs=w_codes[:, keys].bitcast(FP8X4),
@@ -195,22 +201,34 @@ def tile_mixturedenserandomsynthesizer_t_kernel(tc, x_bytes, x_scale, w, rnd, mi
                     start=True,
                     stop=True,
                 )
-            st[("ps", i)] = ps
+            st[("ps", i)] = halves
 
-        def mix_max(i):
+        def blend(i):
             r = i % TILES
-            ps = st.get(("ps", i))
+            halves = st.get(("ps", i))
             logit = work.tile([P, S], F32, name="logit", bufs=3)
+            if i in GPSIMD_MIX:
+                part = work.tile([P, S], F32, name="part")
+                for n in range(2):
+                    keys = slice(n * 512, (n + 1) * 512)
+                    nc.scalar.activation(out=part[:, keys], in_=halves[n][:], func=Act.Copy, scale=mix_f[:, 0:1])
+                nc.gpsimd.tensor_tensor(out=logit[:], in0=part[:], in1=rnd_f[:, r], op=Alu.add)
+                st[("logit", i)] = logit
+                return
             for n in range(2):
                 keys = slice(n * 512, (n + 1) * 512)
                 nc.vector.scalar_tensor_tensor(
                     out=logit[:, keys],
-                    in0=ps[:, n, :],
+                    in0=halves[n][:],
                     scalar=mix_f[:, 0:1],
                     in1=rnd_f[:, r, keys],
                     op0=Alu.mult,
                     op1=Alu.add,
                 )
+            st[("logit", i)] = logit
+
+        def top(i):
+            logit = st.get(("logit", i))
             nmax = work.tile([P, 1], F32, name="nmax", bufs=4)
             nc.vector.tensor_reduce(out=nmax[:], in_=logit[:], axis=AX.X, op=Alu.max, negate=True)
             st[("logit", i)] = (logit, nmax)
@@ -242,6 +260,8 @@ def tile_mixturedenserandomsynthesizer_t_kernel(tc, x_bytes, x_scale, w, rnd, mi
             if i in VECTOR_TILES:
                 e = st.get(("e", i))[0]
                 nc.vector.scalar_tensor_tensor(out=pc[:], in0=e[:], scalar=rinv[:], in1=c_f[:], op0=Alu.mult, op1=Alu.mult)
+            elif i in GPSIMD_NORM:
+                nc.gpsimd.tensor_scalar(out=pc[:], in0=st.get(("ec", i))[:], scalar1=rinv[:], scalar2=1.0, op0=Alu.mult, op1=Alu.mult)
             else:
                 nc.scalar.activation(out=pc[:], in_=st.get(("ec", i))[:], func=Act.Copy, scale=rinv[:])
             st[("pc", i)] = pc
@@ -296,6 +316,8 @@ def tile_mixturedenserandomsynthesizer_t_kernel(tc, x_bytes, x_scale, w, rnd, mi
 
         plan = {}
         late = {}
+        middle = {}
+        early = {}
 
         def put(step, fn, *args):
             plan.setdefault(step, []).append((fn, args))
@@ -307,64 +329,88 @@ def tile_mixturedenserandomsynthesizer_t_kernel(tc, x_bytes, x_scale, w, rnd, mi
                     late.setdefault(8 * b - 4 + k, []).append((x_turn, (b, k)))
                     late.setdefault(8 * b - 3 + k, []).insert(0, (x_second, (b, k)))
                     put(8 * b - 4 + k, x_first, b, k)
-            put(8 * b + 2, v_quantize, b, 0)
+            put(8 * b + 3, v_quantize, b, 0)
             put(8 * b + 4, v_quantize, b, 1)
             for i in range(8):
-                put(8 * b + i // 2, v_bank, b, i // 4, i % 4)
-        for i in range(2, TILES):
-            put(i - 2, rnd_scale, i)
+                step = 8 * b + i // 2 if b > 0 else 2 + i // 4
+                if b > 0 or i % 4 < 2:
+                    early.setdefault(step, []).append((v_product, (b, i // 4, i % 4)))
+                else:
+                    middle.setdefault(step, []).append((v_product, (b, i // 4, i % 4)))
+                middle.setdefault(step, []).append((v_gain, (b, i // 4, i % 4)))
+        for i in range(3, TILES):
+            put(max(2, i - 2), rnd_scale, i)
 
         with tc.manual_schedule():
-            nc.vector.tensor_copy(out=xs[:, D : 2 * D], in_=xs[:, 0:D])
-            rnd_scale(0)
-            rnd_scale(1)
-            nc.gpsimd.tensor_scalar(out=c_f[:], in0=c_b[:], scalar1=1.0, scalar2=0.0, op0=Alu.mult, op1=Alu.add)
             w_grouped = []
             for n in range(2):
                 w_grouped.append(keep.tile([P, 512, PACK], BF16, name="w_grouped%d" % n, align_bytes=64))
             wv_grouped = keep.tile([P, D, PACK], BF16, name="wv_grouped", align_bytes=64)
+            weight_copy(w_raw, 512, slice(0, 512), w_grouped[0], True)
+            weight_copy(w_raw, 512, slice(512, 1024), w_grouped[1], False)
+            nc.vector.tensor_copy(out=xs[:, D : 2 * D], in_=xs[:, 0:D])
+            nc.vector.tensor_copy(out=mix_f[:], in_=mix_b[:])
+            weight_quantize(w_grouped[0], w_codes, w_scales, slice(0, 512))
             x_first(0, 0)
             x_turn(0, 0)
+            nc.vector.tensor_copy(out=u_f[:], in_=u_b[:])
+            x_second(0, 0)
             x_first(0, 1)
             x_turn(0, 1)
-            weight_copy(w_raw, 512, slice(0, 512), w_grouped[0], True)
-            x_second(0, 0)
+            rnd_scale(0)
             x_second(0, 1)
-            weight_copy(w_raw, 512, slice(512, 1024), w_grouped[1], False)
-            x_third(0, 0)
             x_first(0, 2)
+            x_third(0, 0)
+            weight_quantize(w_grouped[1], w_codes, w_scales, slice(512, 1024))
+            syn(0)
             x_turn(0, 2)
-            x_third(0, 1)
+            rnd_scale(1)
+            nc.scalar.copy(out=c_f[:], in_=c_b[:])
             x_second(0, 2)
             x_first(0, 3)
             x_turn(0, 3)
             x_second(0, 3)
-            weight_quantize(w_grouped[0], w_codes, w_scales, slice(0, 512))
-            weight_quantize(w_grouped[1], w_codes, w_scales, slice(512, 1024))
+            blend(0)
+            syn(1)
+            x_third(0, 1)
+            top(0)
+            blend(1)
+            syn(2)
             x_third(0, 2)
+            top(1)
             x_third(0, 3)
             weight_copy(wv_raw, D, slice(0, D), wv_grouped, False)
-            syn(0)
-            mix_max(0)
             weight_quantize(wv_grouped, wv_codes, wv_scales, slice(0, D))
+            exponent(0)
+            gain(0)
+            rnd_scale(2)
 
-            for s in range(N_STEPS + 5):
-                if 1 <= s <= N_STEPS:
+            for s in range(2, N_STEPS + 5):
+                if s <= N_STEPS:
                     exponent(s - 1)
                     gain(s - 1)
-                if s + 1 < N_STEPS and s > 0:
-                    syn(s + 1)
-                if s == 0:
-                    syn(1)
-                if 0 <= s - 2 < N_STEPS:
-                    invert(s - 2)
-                    normalise(s - 2)
                 if 0 <= s - 4 < N_STEPS:
                     p_quantize(s - 4)
                 for fn, args in plan.get(s, []):
                     fn(*args)
+                if s == 2:
+                    invert(0)
+                if 0 <= s - 2 < N_STEPS:
+                    normalise(s - 2)
                 if 0 <= s - 4 < N_STEPS:
                     product(s - 4)
+                for fn, args in early.get(s, []):
+                    fn(*args)
+                if s < N_STEPS:
+                    blend(s)
+                if s + 1 < N_STEPS:
+                    syn(s + 1)
+                for fn, args in middle.get(s, []):
+                    fn(*args)
+                if s <= N_STEPS:
+                    invert(s - 1)
+                if s < N_STEPS:
+                    top(s)
                 if 0 <= s - 2 < N_STEPS:
                     turn(s - 2)
                 if 0 <= s - 3 < N_STEPS:
@@ -373,5 +419,3 @@ def tile_mixturedenserandomsynthesizer_t_kernel(tc, x_bytes, x_scale, w, rnd, mi
                     store(s - 4)
                 for fn, args in late.get(s, []):
                     fn(*args)
-                if 0 < s < N_STEPS:
-                    mix_max(s)

@@ -25,6 +25,7 @@ FLOPS = 2 * B * S * D * S + 2 * B * S * D * D + 2 * B * S * S * D
 VECTOR_TILES = (N_STEPS - 3, N_STEPS - 2, N_STEPS - 1)
 GPSIMD_NORM = ()
 GPSIMD_MIX = ()
+GPSIMD_RND = ()
 
 
 def tile_mixturedenserandomsynthesizer_t_kernel(tc, x_bytes, x_scale, w, rnd, mix, wv, c, u, out):
@@ -37,14 +38,19 @@ def tile_mixturedenserandomsynthesizer_t_kernel(tc, x_bytes, x_scale, w, rnd, mi
         ps_acc = ctx.enter_context(tc.psum_pool(name="ps_acc", bufs=1))
         ps_prep = ctx.enter_context(tc.psum_pool(name="ps_prep", bufs=2))
 
+        x_scale_flat = x_scale.rearrange("a b k -> (a b k)")
+        s4 = keep.tile([P, PACK], F32, name="s4")
+        nc.scalar.dma_start(out=s4[:], in_=x_scale_flat.rearrange("(p t) -> p t", t=PACK))
         xs = keep.tile([P, 2 * D], F32, name="xs")
-        nc.scalar.dma_start(out=xs[:, 0:D], in_=x_scale.rearrange("a b k -> (a b k)").partition_broadcast(P))
         mix_b = keep.tile([P, 2], BF16, name="mix_b")
         nc.scalar.dma_start(out=mix_b[:], in_=mix.partition_broadcast(P))
         u_b = keep.tile([P, H, PACK], BF16, name="u_b")
         nc.scalar.dma_start(out=u_b[:], in_=u.rearrange("(h p t) -> p h t", p=P, t=PACK))
-        c_b = keep.tile([P, S], BF16, name="c_b")
-        nc.scalar.dma_start(out=c_b[:], in_=c.partition_broadcast(P))
+        c_row = keep.tile([P, S], BF16, name="c_row")
+        nc.gpsimd.memset(c_row[:], 0.0)
+        ones = keep.tile([P, P], BF16, name="ones")
+        nc.gpsimd.memset(ones[:], 1.0)
+        nc.scalar.dma_start(out=c_row[0:1, :], in_=c.rearrange("(o k) -> o k", o=1))
 
         xb = []
         for b in range(B):
@@ -59,8 +65,9 @@ def tile_mixturedenserandomsynthesizer_t_kernel(tc, x_bytes, x_scale, w, rnd, mi
         nc.sync.dma_start(out=w_raw[:, :, 0:512], in_=w_v[:, :, 0:512])
         nc.sync.dma_start(out=xb[0][:, 0], in_=xv[0, :, 0])
         nc.sync.dma_start(out=w_raw[:, :, 512:1024], in_=w_v[:, :, 512:1024])
-        nc.sync.dma_start(out=xb[0][:, 1], in_=xv[0, :, 1])
         nc.sync.dma_start(out=rnd_raw[:, 0:2], in_=rnd_v[:, 0, 0:2])
+        nc.sync.dma_start(out=xb[0][:, 1], in_=xv[0, :, 1])
+        nc.sync.dma_start(out=xs[:, 0:D], in_=x_scale_flat.partition_broadcast(P))
         nc.sync.dma_start(out=wv_raw[:], in_=wv.rearrange("(p j) n -> p j n", j=PACK))
         nc.sync.dma_start(out=rnd_raw[:, 2:4], in_=rnd_v[:, 0, 2:4])
         nc.sync.dma_start(out=rnd_raw[:, 4:8], in_=rnd_v[:, 1])
@@ -91,7 +98,10 @@ def tile_mixturedenserandomsynthesizer_t_kernel(tc, x_bytes, x_scale, w, rnd, mi
         out_v = out.rearrange("b (h m t) d -> b m h t d", m=P, t=PACK)
 
         def rnd_scale(i):
-            nc.scalar.activation(out=rnd_f[:, i], in_=rnd_raw[:, i], func=Act.Copy, scale=mix_f[:, 1:2])
+            if i in GPSIMD_RND:
+                nc.gpsimd.tensor_scalar(out=rnd_f[:, i], in0=rnd_raw[:, i], scalar1=mix_f[:, 1:2], scalar2=0.0, op0=Alu.mult, op1=Alu.add)
+            else:
+                nc.scalar.activation(out=rnd_f[:, i], in_=rnd_raw[:, i], func=Act.Copy, scale=mix_f[:, 1:2])
 
         def weight_copy(raw, width, cols, grouped, on_vector):
             src = raw[:, :, cols].rearrange("p j n -> p n j")
@@ -108,6 +118,30 @@ def tile_mixturedenserandomsynthesizer_t_kernel(tc, x_bytes, x_scale, w, rnd, mi
             )
 
         x_state = {}
+
+        def x_widen(b, k):
+            h, t = k // 2, 2 * (k % 2)
+            xw = work.tile([P, 2 * D], BF16, name="xw")
+            nc.scalar.copy(out=xw[:], in_=xb[b][:, h, t : t + 2, :].rearrange("p t k -> p (t k)").bitcast(FP8))
+            x_state[(b, k)] = xw
+
+        def x_scale_out(b, k):
+            tr = x_state.get((b, k))
+            xg = work.tile([P, 2, P, PACK], BF16, name="xg", align_bytes=64)
+            for j in range(2):
+                nc.vector.tensor_tensor(
+                    out=xg[:, j].rearrange("p q (u e) -> p q u e", e=2),
+                    in0=tr[:, j].rearrange("p u q -> p (u q)").bitcast(BF16).rearrange("p (u q e) -> p q u e", u=2, e=2),
+                    in1=s4[:].rearrange("p (o u e) -> p o u e", o=1, e=2).to_broadcast([P, P, 2, 2]),
+                    op=Alu.mult,
+                )
+            x_state[(b, k)] = xg
+
+        def c_spread():
+            for n in range(2):
+                acc = ps_prep.tile([P, 512], F32, name="prep")
+                nc.tensor.matmul(acc[:], lhsT=ones[:], rhs=c_row[:, n * 512 : (n + 1) * 512], start=True, stop=True)
+                nc.scalar.copy(out=c_f[:, n * 512 : (n + 1) * 512], in_=acc[:])
 
         def x_first(b, k):
             h, t = k // 2, 2 * (k % 2)
@@ -318,6 +352,7 @@ def tile_mixturedenserandomsynthesizer_t_kernel(tc, x_bytes, x_scale, w, rnd, mi
         late = {}
         middle = {}
         early = {}
+        extra = {}
 
         def put(step, fn, *args):
             plan.setdefault(step, []).append((fn, args))
@@ -339,7 +374,7 @@ def tile_mixturedenserandomsynthesizer_t_kernel(tc, x_bytes, x_scale, w, rnd, mi
                     middle.setdefault(step, []).append((v_product, (b, i // 4, i % 4)))
                 middle.setdefault(step, []).append((v_gain, (b, i // 4, i % 4)))
         for i in range(3, TILES):
-            put(max(2, i - 2), rnd_scale, i)
+            extra.setdefault(max(2, i - 2), []).append((rnd_scale, (i,)))
 
         with tc.manual_schedule():
             w_grouped = []
@@ -347,43 +382,42 @@ def tile_mixturedenserandomsynthesizer_t_kernel(tc, x_bytes, x_scale, w, rnd, mi
                 w_grouped.append(keep.tile([P, 512, PACK], BF16, name="w_grouped%d" % n, align_bytes=64))
             wv_grouped = keep.tile([P, D, PACK], BF16, name="wv_grouped", align_bytes=64)
             weight_copy(w_raw, 512, slice(0, 512), w_grouped[0], True)
-            weight_copy(w_raw, 512, slice(512, 1024), w_grouped[1], False)
-            nc.vector.tensor_copy(out=xs[:, D : 2 * D], in_=xs[:, 0:D])
-            nc.vector.tensor_copy(out=mix_f[:], in_=mix_b[:])
-            weight_quantize(w_grouped[0], w_codes, w_scales, slice(0, 512))
-            x_first(0, 0)
+            x_widen(0, 0)
             x_turn(0, 0)
+            weight_quantize(w_grouped[0], w_codes, w_scales, slice(0, 512))
+            nc.vector.tensor_copy(out=mix_f[:], in_=mix_b[:])
             nc.vector.tensor_copy(out=u_f[:], in_=u_b[:])
-            x_second(0, 0)
-            x_first(0, 1)
+            weight_copy(w_raw, 512, slice(512, 1024), w_grouped[1], True)
+            x_widen(0, 1)
             x_turn(0, 1)
+            x_scale_out(0, 0)
             rnd_scale(0)
-            x_second(0, 1)
-            x_first(0, 2)
-            x_third(0, 0)
             weight_quantize(w_grouped[1], w_codes, w_scales, slice(512, 1024))
+            x_scale_out(0, 1)
+            x_third(0, 0)
             syn(0)
-            x_turn(0, 2)
+            x_third(0, 1)
             rnd_scale(1)
-            nc.scalar.copy(out=c_f[:], in_=c_b[:])
-            x_second(0, 2)
-            x_first(0, 3)
-            x_turn(0, 3)
-            x_second(0, 3)
+            c_spread()
+            weight_copy(wv_raw, D, slice(0, D), wv_grouped, False)
+            nc.vector.tensor_copy(out=xs[:, D : 2 * D], in_=xs[:, 0:D])
             blend(0)
             syn(1)
-            x_third(0, 1)
+            x_first(0, 2)
+            x_turn(0, 2)
             top(0)
+            x_first(0, 3)
+            x_turn(0, 3)
+            x_second(0, 2)
             blend(1)
             syn(2)
-            x_third(0, 2)
-            top(1)
-            x_third(0, 3)
-            weight_copy(wv_raw, D, slice(0, D), wv_grouped, False)
-            weight_quantize(wv_grouped, wv_codes, wv_scales, slice(0, D))
+            rnd_scale(2)
+            x_second(0, 3)
             exponent(0)
             gain(0)
-            rnd_scale(2)
+            top(1)
+            x_third(0, 2)
+            x_third(0, 3)
 
             for s in range(2, N_STEPS + 5):
                 if s <= N_STEPS:
@@ -394,9 +428,12 @@ def tile_mixturedenserandomsynthesizer_t_kernel(tc, x_bytes, x_scale, w, rnd, mi
                 for fn, args in plan.get(s, []):
                     fn(*args)
                 if s == 2:
+                    weight_quantize(wv_grouped, wv_codes, wv_scales, slice(0, D))
                     invert(0)
                 if 0 <= s - 2 < N_STEPS:
                     normalise(s - 2)
+                for fn, args in extra.get(s, []):
+                    fn(*args)
                 if 0 <= s - 4 < N_STEPS:
                     product(s - 4)
                 for fn, args in early.get(s, []):

@@ -34,9 +34,9 @@ def tile_mixturedenserandomsynthesizer_t_kernel(tc, x_bytes, x_scale, w, rnd, mi
         keep = ctx.enter_context(tc.tile_pool(name="keep", bufs=1))
         work = ctx.enter_context(tc.tile_pool(name="work", bufs=2))
         ps_syn = ctx.enter_context(tc.psum_pool(name="ps_syn", bufs=3))
-        ps_tr = ctx.enter_context(tc.psum_pool(name="ps_tr", bufs=2))
+        ps_tr = ctx.enter_context(tc.psum_pool(name="ps_tr", bufs=1))
         ps_acc = ctx.enter_context(tc.psum_pool(name="ps_acc", bufs=1))
-        ps_prep = ctx.enter_context(tc.psum_pool(name="ps_prep", bufs=2))
+        ps_prep = ctx.enter_context(tc.psum_pool(name="ps_prep", bufs=3))
 
         x_scale_flat = x_scale.rearrange("a b k -> (a b k)")
         s4 = keep.tile([P, PACK], F32, name="s4")
@@ -98,10 +98,14 @@ def tile_mixturedenserandomsynthesizer_t_kernel(tc, x_bytes, x_scale, w, rnd, mi
         out_v = out.rearrange("b (h m t) d -> b m h t d", m=P, t=PACK)
 
         def rnd_scale(i):
-            if i in GPSIMD_RND:
-                nc.gpsimd.tensor_scalar(out=rnd_f[:, i], in0=rnd_raw[:, i], scalar1=mix_f[:, 1:2], scalar2=0.0, op0=Alu.mult, op1=Alu.add)
-            else:
-                nc.scalar.activation(out=rnd_f[:, i], in_=rnd_raw[:, i], func=Act.Copy, scale=mix_f[:, 1:2])
+            for n in range(2):
+                keys = slice(n * 512, (n + 1) * 512)
+                nc.scalar.activation(
+                    out=rnd_f[:, i, keys].rearrange("p (u m e) -> p u m e", u=2, e=2),
+                    in_=rnd_raw[:, i, keys].rearrange("p (m u e) -> p u m e", u=2, e=2),
+                    func=Act.Copy,
+                    scale=mix_f[:, 1:2],
+                )
 
         def weight_copy(raw, width, cols, grouped, on_vector):
             src = raw[:, :, cols].rearrange("p j n -> p n j")
@@ -109,6 +113,12 @@ def tile_mixturedenserandomsynthesizer_t_kernel(tc, x_bytes, x_scale, w, rnd, mi
                 nc.vector.tensor_copy(out=grouped[:], in_=src)
             else:
                 nc.scalar.copy(out=grouped[:], in_=src)
+
+        def w_copy(n):
+            src = w_raw[:, :, n * 512 : (n + 1) * 512].rearrange("p j (m u e) -> p u m e j", u=2, e=2)
+            dst = w_grouped[n][:].rearrange("p (u m e) j -> p u m e j", u=2, e=2)
+            for u_half in range(2):
+                nc.vector.tensor_copy(out=dst[:, u_half], in_=src[:, u_half])
 
         def weight_quantize(grouped, codes, scales, cols):
             nc.vector.quantize_mx(
@@ -141,7 +151,10 @@ def tile_mixturedenserandomsynthesizer_t_kernel(tc, x_bytes, x_scale, w, rnd, mi
             for n in range(2):
                 acc = ps_prep.tile([P, 512], F32, name="prep")
                 nc.tensor.matmul(acc[:], lhsT=ones[:], rhs=c_row[:, n * 512 : (n + 1) * 512], start=True, stop=True)
-                nc.scalar.copy(out=c_f[:, n * 512 : (n + 1) * 512], in_=acc[:])
+                nc.scalar.copy(
+                    out=c_f[:, n * 512 : (n + 1) * 512].rearrange("p (u m e) -> p u m e", u=2, e=2),
+                    in_=acc[:].rearrange("p (m u e) -> p u m e", u=2, e=2),
+                )
 
         def x_first(b, k):
             h, t = k // 2, 2 * (k % 2)
@@ -306,7 +319,8 @@ def tile_mixturedenserandomsynthesizer_t_kernel(tc, x_bytes, x_scale, w, rnd, mi
             tr = ps_tr.tile([P, 2, 2, P], F32, name="tr")
             for g in range(2):
                 for e in range(2):
-                    nc.tensor.transpose(tr[:, g, e, :], words[:, 256 * g + e : 256 * (g + 1) : 2], ident[:])
+                    first = 256 * g + P * e
+                    nc.tensor.transpose(tr[:, g, e, :], words[:, first : first + P], ident[:])
             st[("tr", i)] = tr
 
         def turn_out(i):
@@ -329,7 +343,10 @@ def tile_mixturedenserandomsynthesizer_t_kernel(tc, x_bytes, x_scale, w, rnd, mi
         def product(i):
             b = i // TILES
             p_codes, p_scales = st.get(("p", i))
-            acc = ps_acc.tile([P, D], F32, name="acc")
+            if i < N_STEPS - 4:
+                acc = ps_acc.tile([P, D], F32, name="acc")
+            else:
+                acc = ps_prep.tile([P, D], F32, name="prep")
             for g in range(2):
                 nc.tensor.matmul_mx(
                     out=acc[:],
@@ -352,6 +369,7 @@ def tile_mixturedenserandomsynthesizer_t_kernel(tc, x_bytes, x_scale, w, rnd, mi
         late = {}
         middle = {}
         early = {}
+        second = {}
         extra = {}
 
         def put(step, fn, *args):
@@ -362,13 +380,15 @@ def tile_mixturedenserandomsynthesizer_t_kernel(tc, x_bytes, x_scale, w, rnd, mi
                 for k in range(4):
                     put(8 * b - 2 + k, x_third, b, k)
                     late.setdefault(8 * b - 4 + k, []).append((x_turn, (b, k)))
-                    late.setdefault(8 * b - 3 + k, []).insert(0, (x_second, (b, k)))
+                    second.setdefault(8 * b - 3 + k, []).append((x_second, (b, k)))
                     put(8 * b - 4 + k, x_first, b, k)
             put(8 * b + 3, v_quantize, b, 0)
             put(8 * b + 4, v_quantize, b, 1)
             for i in range(8):
                 step = 8 * b + i // 2 if b > 0 else 2 + i // 4
-                if b > 0 or i % 4 < 2:
+                if b > 0:
+                    late.setdefault(step - 1, []).append((v_product, (b, i // 4, i % 4)))
+                elif i % 4 < 2:
                     early.setdefault(step, []).append((v_product, (b, i // 4, i % 4)))
                 else:
                     middle.setdefault(step, []).append((v_product, (b, i // 4, i % 4)))
@@ -381,13 +401,13 @@ def tile_mixturedenserandomsynthesizer_t_kernel(tc, x_bytes, x_scale, w, rnd, mi
             for n in range(2):
                 w_grouped.append(keep.tile([P, 512, PACK], BF16, name="w_grouped%d" % n, align_bytes=64))
             wv_grouped = keep.tile([P, D, PACK], BF16, name="wv_grouped", align_bytes=64)
-            weight_copy(w_raw, 512, slice(0, 512), w_grouped[0], True)
+            w_copy(0)
             x_widen(0, 0)
             x_turn(0, 0)
             weight_quantize(w_grouped[0], w_codes, w_scales, slice(0, 512))
             nc.vector.tensor_copy(out=mix_f[:], in_=mix_b[:])
             nc.vector.tensor_copy(out=u_f[:], in_=u_b[:])
-            weight_copy(w_raw, 512, slice(512, 1024), w_grouped[1], True)
+            w_copy(1)
             x_widen(0, 1)
             x_turn(0, 1)
             x_scale_out(0, 0)
@@ -423,6 +443,10 @@ def tile_mixturedenserandomsynthesizer_t_kernel(tc, x_bytes, x_scale, w, rnd, mi
                 if s <= N_STEPS:
                     exponent(s - 1)
                     gain(s - 1)
+                for fn, args in second.get(s, []):
+                    fn(*args)
+                if 0 <= s - 3 < N_STEPS:
+                    turn_out(s - 3)
                 if 0 <= s - 4 < N_STEPS:
                     p_quantize(s - 4)
                 for fn, args in plan.get(s, []):
@@ -450,8 +474,6 @@ def tile_mixturedenserandomsynthesizer_t_kernel(tc, x_bytes, x_scale, w, rnd, mi
                     top(s)
                 if 0 <= s - 2 < N_STEPS:
                     turn(s - 2)
-                if 0 <= s - 3 < N_STEPS:
-                    turn_out(s - 3)
                 if 0 <= s - 4 < N_STEPS:
                     store(s - 4)
                 for fn, args in late.get(s, []):

@@ -6,9 +6,11 @@ from concourse.masks import make_identity
 B, S, D = 4, 1024, 512
 P = 128
 PACK = 4
-H = S // (P * PACK)
+HALF = P * PACK
+HALVES = S // HALF
 TILES = S // P
-N_STEPS = B * TILES
+N_TILES = B * TILES
+BANK = 512
 
 F32 = mybir.dt.float32
 BF16 = mybir.dt.bfloat16
@@ -22,10 +24,9 @@ AX = mybir.AxisListType
 
 FLOPS = 2 * B * S * D * S + 2 * B * S * D * D + 2 * B * S * S * D
 
-VECTOR_TILES = (N_STEPS - 3, N_STEPS - 2, N_STEPS - 1)
-GPSIMD_NORM = ()
-GPSIMD_MIX = ()
-GPSIMD_RND = ()
+VECTOR_TILES = (N_TILES - 3, N_TILES - 2, N_TILES - 1)
+
+SPARE_BANK_TILES = range(N_TILES - 4, N_TILES)
 
 
 def tile_mixturedenserandomsynthesizer_t_kernel(tc, x_bytes, x_scale, w, rnd, mix, wv, c, u, out):
@@ -33,46 +34,46 @@ def tile_mixturedenserandomsynthesizer_t_kernel(tc, x_bytes, x_scale, w, rnd, mi
     with ExitStack() as ctx:
         keep = ctx.enter_context(tc.tile_pool(name="keep", bufs=1))
         work = ctx.enter_context(tc.tile_pool(name="work", bufs=2))
-        ps_syn = ctx.enter_context(tc.psum_pool(name="ps_syn", bufs=3))
-        ps_tr = ctx.enter_context(tc.psum_pool(name="ps_tr", bufs=1))
-        ps_acc = ctx.enter_context(tc.psum_pool(name="ps_acc", bufs=1))
+        ps_score = ctx.enter_context(tc.psum_pool(name="ps_score", bufs=3))
+        ps_turn = ctx.enter_context(tc.psum_pool(name="ps_turn", bufs=1))
+        ps_sum = ctx.enter_context(tc.psum_pool(name="ps_sum", bufs=1))
         ps_prep = ctx.enter_context(tc.psum_pool(name="ps_prep", bufs=3))
 
         x_scale_flat = x_scale.rearrange("a b k -> (a b k)")
-        s4 = keep.tile([P, PACK], F32, name="s4")
-        nc.scalar.dma_start(out=s4[:], in_=x_scale_flat.rearrange("(p t) -> p t", t=PACK))
-        xs = keep.tile([P, 2 * D], F32, name="xs")
-        mix_b = keep.tile([P, 2], BF16, name="mix_b")
-        nc.scalar.dma_start(out=mix_b[:], in_=mix.partition_broadcast(P))
-        u_b = keep.tile([P, H, PACK], BF16, name="u_b")
-        nc.scalar.dma_start(out=u_b[:], in_=u.rearrange("(h p t) -> p h t", p=P, t=PACK))
+        scale_4 = keep.tile([P, PACK], F32, name="scale_4")
+        nc.scalar.dma_start(out=scale_4[:], in_=x_scale_flat.rearrange("(p t) -> p t", t=PACK))
+        mix_raw = keep.tile([P, 2], BF16, name="mix_raw")
+        nc.scalar.dma_start(out=mix_raw[:], in_=mix.partition_broadcast(P))
+        u_raw = keep.tile([P, HALVES, PACK], BF16, name="u_raw")
+        nc.scalar.dma_start(out=u_raw[:], in_=u.rearrange("(h p t) -> p h t", p=P, t=PACK))
         c_row = keep.tile([P, S], BF16, name="c_row")
         nc.gpsimd.memset(c_row[:], 0.0)
         ones = keep.tile([P, P], BF16, name="ones")
         nc.gpsimd.memset(ones[:], 1.0)
         nc.scalar.dma_start(out=c_row[0:1, :], in_=c.rearrange("(o k) -> o k", o=1))
 
-        xb = []
+        x_rows = x_bytes.rearrange("b (h m t) k -> b m h t k", m=P, t=PACK)
+        x_raw = []
         for b in range(B):
-            xb.append(keep.tile([P, H, PACK, D], U8, name="xb%d" % b, align_bytes=64))
-        xv = x_bytes.rearrange("b (h m t) k -> b m h t k", m=P, t=PACK)
+            x_raw.append(keep.tile([P, HALVES, PACK, D], U8, name="x_raw%d" % b, align_bytes=64))
+        rnd_rows = rnd.rearrange("(h m t) k -> m h t k", m=P, t=PACK)
+        rnd_raw = keep.tile([P, TILES, S], BF16, name="rnd_raw")
+        w_rows = w.rearrange("(p j) n -> p j n", j=PACK)
         w_raw = keep.tile([P, PACK, S], BF16, name="w_raw")
         wv_raw = keep.tile([P, PACK, D], BF16, name="wv_raw")
-        rnd_raw = keep.tile([P, TILES, S], BF16, name="rnd_raw")
-        rnd_v = rnd.rearrange("(h m t) k -> m h t k", m=P, t=PACK)
-        w_v = w.rearrange("(p j) n -> p j n", j=PACK)
+        scale_row = keep.tile([P, 2 * D], F32, name="scale_row")
 
-        nc.sync.dma_start(out=w_raw[:, :, 0:512], in_=w_v[:, :, 0:512])
-        nc.sync.dma_start(out=xb[0][:, 0], in_=xv[0, :, 0])
-        nc.sync.dma_start(out=w_raw[:, :, 512:1024], in_=w_v[:, :, 512:1024])
-        nc.sync.dma_start(out=rnd_raw[:, 0:2], in_=rnd_v[:, 0, 0:2])
-        nc.sync.dma_start(out=xb[0][:, 1], in_=xv[0, :, 1])
-        nc.sync.dma_start(out=xs[:, 0:D], in_=x_scale_flat.partition_broadcast(P))
+        nc.sync.dma_start(out=w_raw[:, :, 0:BANK], in_=w_rows[:, :, 0:BANK])
+        nc.sync.dma_start(out=x_raw[0][:, 0], in_=x_rows[0, :, 0])
+        nc.sync.dma_start(out=w_raw[:, :, BANK:S], in_=w_rows[:, :, BANK:S])
+        nc.sync.dma_start(out=rnd_raw[:, 0:2], in_=rnd_rows[:, 0, 0:2])
+        nc.sync.dma_start(out=x_raw[0][:, 1], in_=x_rows[0, :, 1])
+        nc.sync.dma_start(out=scale_row[:, 0:D], in_=x_scale_flat.partition_broadcast(P))
         nc.sync.dma_start(out=wv_raw[:], in_=wv.rearrange("(p j) n -> p j n", j=PACK))
-        nc.sync.dma_start(out=rnd_raw[:, 2:4], in_=rnd_v[:, 0, 2:4])
-        nc.sync.dma_start(out=rnd_raw[:, 4:8], in_=rnd_v[:, 1])
+        nc.sync.dma_start(out=rnd_raw[:, 2:4], in_=rnd_rows[:, 0, 2:4])
+        nc.sync.dma_start(out=rnd_raw[:, 4:8], in_=rnd_rows[:, 1])
         for b in range(1, B):
-            nc.sync.dma_start(out=xb[b][:], in_=xv[b])
+            nc.sync.dma_start(out=x_raw[b][:], in_=x_rows[b])
 
         ident = keep.tile([P, P], F32, name="ident")
         make_identity(nc, ident[:])
@@ -80,10 +81,14 @@ def tile_mixturedenserandomsynthesizer_t_kernel(tc, x_bytes, x_scale, w, rnd, mi
         nc.vector.memset(warm[:], 0.0)
         nc.scalar.activation(out=warm[:], in_=warm[:], func=Act.Exp)
         mix_f = keep.tile([P, 2], F32, name="mix_f")
-        u_f = keep.tile([P, H, PACK], F32, name="u_f")
+        u_f = keep.tile([P, HALVES, PACK], F32, name="u_f")
         c_f = keep.tile([P, S], F32, name="c_f")
         rnd_f = keep.tile([P, TILES, S], F32, name="rnd_f")
 
+        w_grouped = []
+        for g in range(HALVES):
+            w_grouped.append(keep.tile([P, BANK, PACK], BF16, name="w_grouped%d" % g, align_bytes=64))
+        wv_grouped = keep.tile([P, D, PACK], BF16, name="wv_grouped", align_bytes=64)
         w_codes = keep.tile([P, S], U32, name="w_codes", align_bytes=64)
         w_scales = keep.tile([P, S], U8, name="w_scales", align_bytes=64)
         wv_codes = keep.tile([P, D], U32, name="wv_codes", align_bytes=64)
@@ -92,389 +97,365 @@ def tile_mixturedenserandomsynthesizer_t_kernel(tc, x_bytes, x_scale, w, rnd, mi
         for b in range(B):
             x_codes.append(keep.tile([P, S], U32, name="x_codes%d" % b, align_bytes=64))
             x_scales.append(keep.tile([P, S], U8, name="x_scales%d" % b, align_bytes=64))
-            v_codes.append(keep.tile([P, H, D], U32, name="v_codes%d" % b, align_bytes=64))
-            v_scales.append(keep.tile([P, H, D], U8, name="v_scales%d" % b, align_bytes=64))
+            v_codes.append(keep.tile([P, HALVES, D], U32, name="v_codes%d" % b, align_bytes=64))
+            v_scales.append(keep.tile([P, HALVES, D], U8, name="v_scales%d" % b, align_bytes=64))
 
-        out_v = out.rearrange("b (h m t) d -> b m h t d", m=P, t=PACK)
+        out_rows = out.rearrange("b (h m t) d -> b m h t d", m=P, t=PACK)
 
-        def rnd_scale(i):
-            for n in range(2):
-                keys = slice(n * 512, (n + 1) * 512)
+        def key_columns(ap):
+            return ap.rearrange("p (m h e) -> p h m e", h=2, e=2)
+
+        def columns_split(ap):
+            return ap.rearrange("p (h m e) -> p h m e", h=2, e=2)
+
+        def w_group(g):
+            src = w_raw[:, :, g * BANK : (g + 1) * BANK].rearrange("p j (m h e) -> p h m e j", h=2, e=2)
+            dst = w_grouped[g][:].rearrange("p (h m e) j -> p h m e j", h=2, e=2)
+            for h in range(2):
+                nc.vector.tensor_copy(out=dst[:, h], in_=src[:, h])
+
+        def w_quantize(g):
+            cols = slice(g * BANK, (g + 1) * BANK)
+            nc.vector.quantize_mx(
+                out=w_codes[:, cols].bitcast(FP8X4),
+                scales=w_scales[:, cols],
+                in_=w_grouped[g][:].rearrange("p n j -> p (n j)"),
+            )
+
+        def wv_group():
+            nc.scalar.copy(out=wv_grouped[:], in_=wv_raw[:].rearrange("p j n -> p n j"))
+
+        def wv_quantize():
+            nc.vector.quantize_mx(
+                out=wv_codes[:].bitcast(FP8X4),
+                scales=wv_scales[:],
+                in_=wv_grouped[:].rearrange("p n j -> p (n j)"),
+            )
+
+        def rnd_scale(r):
+            for g in range(HALVES):
+                cols = slice(g * BANK, (g + 1) * BANK)
                 nc.scalar.activation(
-                    out=rnd_f[:, i, keys].rearrange("p (u m e) -> p u m e", u=2, e=2),
-                    in_=rnd_raw[:, i, keys].rearrange("p (m u e) -> p u m e", u=2, e=2),
+                    out=columns_split(rnd_f[:, r, cols]),
+                    in_=key_columns(rnd_raw[:, r, cols]),
                     func=Act.Copy,
                     scale=mix_f[:, 1:2],
                 )
 
-        def weight_copy(raw, width, cols, grouped, on_vector):
-            src = raw[:, :, cols].rearrange("p j n -> p n j")
-            if on_vector:
-                nc.vector.tensor_copy(out=grouped[:], in_=src)
-            else:
-                nc.scalar.copy(out=grouped[:], in_=src)
-
-        def w_copy(n):
-            src = w_raw[:, :, n * 512 : (n + 1) * 512].rearrange("p j (m u e) -> p u m e j", u=2, e=2)
-            dst = w_grouped[n][:].rearrange("p (u m e) j -> p u m e j", u=2, e=2)
-            for u_half in range(2):
-                nc.vector.tensor_copy(out=dst[:, u_half], in_=src[:, u_half])
-
-        def weight_quantize(grouped, codes, scales, cols):
-            nc.vector.quantize_mx(
-                out=codes[:, cols].bitcast(FP8X4),
-                scales=scales[:, cols],
-                in_=grouped[:].rearrange("p n j -> p (n j)"),
-            )
-
-        x_state = {}
-
-        def x_widen(b, k):
-            h, t = k // 2, 2 * (k % 2)
-            xw = work.tile([P, 2 * D], BF16, name="xw")
-            nc.scalar.copy(out=xw[:], in_=xb[b][:, h, t : t + 2, :].rearrange("p t k -> p (t k)").bitcast(FP8))
-            x_state[(b, k)] = xw
-
-        def x_scale_out(b, k):
-            tr = x_state.get((b, k))
-            xg = work.tile([P, 2, P, PACK], BF16, name="xg", align_bytes=64)
-            for j in range(2):
-                nc.vector.tensor_tensor(
-                    out=xg[:, j].rearrange("p q (u e) -> p q u e", e=2),
-                    in0=tr[:, j].rearrange("p u q -> p (u q)").bitcast(BF16).rearrange("p (u q e) -> p q u e", u=2, e=2),
-                    in1=s4[:].rearrange("p (o u e) -> p o u e", o=1, e=2).to_broadcast([P, P, 2, 2]),
-                    op=Alu.mult,
-                )
-            x_state[(b, k)] = xg
-
         def c_spread():
-            for n in range(2):
-                acc = ps_prep.tile([P, 512], F32, name="prep")
-                nc.tensor.matmul(acc[:], lhsT=ones[:], rhs=c_row[:, n * 512 : (n + 1) * 512], start=True, stop=True)
-                nc.scalar.copy(
-                    out=c_f[:, n * 512 : (n + 1) * 512].rearrange("p (u m e) -> p u m e", u=2, e=2),
-                    in_=acc[:].rearrange("p (m u e) -> p u m e", u=2, e=2),
-                )
+            for g in range(HALVES):
+                cols = slice(g * BANK, (g + 1) * BANK)
+                spread = ps_prep.tile([P, BANK], F32, name="prep")
+                nc.tensor.matmul(spread[:], lhsT=ones[:], rhs=c_row[:, cols], start=True, stop=True)
+                nc.scalar.copy(out=columns_split(c_f[:, cols]), in_=key_columns(spread[:]))
 
-        def x_first(b, k):
+        x_wide, x_turned, x_grouped = {}, {}, {}
+
+        def x_codes_of(b, k):
             h, t = k // 2, 2 * (k % 2)
-            xw = work.tile([P, 2 * D], BF16, name="xw")
-            nc.vector.tensor_tensor(
-                out=xw[:],
-                in0=xb[b][:, h, t : t + 2, :].rearrange("p t k -> p (t k)").bitcast(FP8),
-                in1=xs[:],
-                op=Alu.mult,
-            )
-            x_state[(b, k)] = xw
+            return x_raw[b][:, h, t : t + 2, :].rearrange("p t k -> p (t k)").bitcast(FP8)
+
+        def x_scaled(b, k):
+            wide = work.tile([P, 2 * D], BF16, name="wide")
+            nc.vector.tensor_tensor(out=wide[:], in0=x_codes_of(b, k), in1=scale_row[:], op=Alu.mult)
+            x_wide[(b, k)] = wide
+
+        def x_plain(b, k):
+            wide = work.tile([P, 2 * D], BF16, name="wide")
+            nc.scalar.copy(out=wide[:], in_=x_codes_of(b, k))
+            x_wide[(b, k)] = wide
 
         def x_turn(b, k):
-            words = x_state.get((b, k))[:].bitcast(F32)
-            tr = ps_prep.tile([P, 2, 2, P], F32, name="prep")
+            words = x_wide.get((b, k))[:].bitcast(F32)
+            turned = ps_prep.tile([P, 2, 2, P], F32, name="prep")
             for j in range(2):
                 for e in range(2):
-                    nc.tensor.transpose(tr[:, j, e, :], words[:, 256 * j + e : 256 * (j + 1) : 2], ident[:])
-            x_state[(b, k)] = tr
+                    nc.tensor.transpose(turned[:, j, e, :], words[:, 256 * j + e : 256 * (j + 1) : 2], ident[:])
+            x_turned[(b, k)] = turned
 
-        def x_second(b, k):
-            tr = x_state.get((b, k))
-            xg = work.tile([P, 2, P, PACK], BF16, name="xg", align_bytes=64)
-            nc.scalar.copy(out=xg[:].bitcast(F32), in_=tr[:].rearrange("p j e q -> p j q e"))
-            x_state[(b, k)] = xg
+        def x_copy_out(b, k):
+            grouped = work.tile([P, 2, P, PACK], BF16, name="x_grouped", align_bytes=64)
+            nc.scalar.copy(
+                out=grouped[:].bitcast(F32), in_=x_turned.get((b, k))[:].rearrange("p j e q -> p j q e")
+            )
+            x_grouped[(b, k)] = grouped
 
-        def x_third(b, k):
-            xg = x_state.get((b, k))
-            cols = slice(256 * k, 256 * (k + 1))
+        def x_scaled_late(b, k):
+            turned = x_turned.get((b, k))
+            grouped = work.tile([P, 2, P, PACK], BF16, name="x_grouped", align_bytes=64)
+            for j in range(2):
+                nc.vector.tensor_tensor(
+                    out=grouped[:, j].rearrange("p q (h e) -> p q h e", e=2),
+                    in0=turned[:, j]
+                    .rearrange("p h q -> p (h q)")
+                    .bitcast(BF16)
+                    .rearrange("p (h q e) -> p q h e", h=2, e=2),
+                    in1=scale_4[:].rearrange("p (o h e) -> p o h e", o=1, e=2).to_broadcast([P, P, 2, 2]),
+                    op=Alu.mult,
+                )
+            x_grouped[(b, k)] = grouped
+
+        def x_quantize(b, k):
+            cols = slice(2 * P * k, 2 * P * (k + 1))
             nc.vector.quantize_mx(
                 out=x_codes[b][:, cols].bitcast(FP8X4),
                 scales=x_scales[b][:, cols],
-                in_=xg[:].rearrange("p j q t -> p (j q t)"),
+                in_=x_grouped.get((b, k))[:].rearrange("p j q t -> p (j q t)"),
             )
 
-        v_state = {}
+        v_sums, v_grouped = {}, {}
 
-        def v_product(b, h, dj):
-            acc = ps_prep.tile([P, PACK, P], F32, name="prep")
-            d_cols = slice(dj * P, (dj + 1) * P)
+        def v_product(b, h, n):
+            sums = ps_prep.tile([P, PACK, P], F32, name="prep")
+            d_cols = slice(n * P, (n + 1) * P)
             for t in range(PACK):
-                r_cols = slice((h * PACK + t) * P, (h * PACK + t + 1) * P)
+                rows = slice((h * PACK + t) * P, (h * PACK + t + 1) * P)
                 nc.tensor.matmul_mx(
-                    out=acc[:, t, :],
-                    lhsT=x_codes[b][:, r_cols].bitcast(FP8X4),
-                    lhsT_scale=x_scales[b][:, r_cols],
+                    out=sums[:, t, :],
+                    lhsT=x_codes[b][:, rows].bitcast(FP8X4),
+                    lhsT_scale=x_scales[b][:, rows],
                     rhs=wv_codes[:, d_cols].bitcast(FP8X4),
                     rhs_scale=wv_scales[:, d_cols],
                     start=True,
                     stop=True,
                 )
-            v_state[(b, h, dj)] = acc
+            v_sums[(b, h, n)] = sums
 
-        def v_gain(b, h, dj):
-            if dj == 0:
-                v_state[(b, h)] = work.tile([P, D, PACK], BF16, name="vg", align_bytes=64)
-            vg = v_state.get((b, h))
-            acc = v_state.get((b, h, dj))
-            d_cols = slice(dj * P, (dj + 1) * P)
+        def v_gain(b, h, n):
+            if n == 0:
+                v_grouped[(b, h)] = work.tile([P, D, PACK], BF16, name="v_grouped", align_bytes=64)
             nc.vector.tensor_tensor(
-                out=vg[:, d_cols, :],
-                in0=acc[:].rearrange("p t d -> p d t"),
+                out=v_grouped.get((b, h))[:, n * P : (n + 1) * P, :],
+                in0=v_sums.get((b, h, n))[:].rearrange("p t d -> p d t"),
                 in1=u_f[:, h : h + 1, :].to_broadcast([P, P, PACK]),
                 op=Alu.mult,
             )
 
         def v_quantize(b, h):
-            vg = v_state.get((b, h))
             nc.vector.quantize_mx(
                 out=v_codes[b][:, h, :].bitcast(FP8X4),
                 scales=v_scales[b][:, h, :],
-                in_=vg[:].rearrange("p d t -> p (d t)"),
+                in_=v_grouped.get((b, h))[:].rearrange("p d t -> p (d t)"),
             )
 
-        st = {}
+        scores, logits, maxima, exps, totals, inverses = {}, {}, {}, {}, {}, {}
+        gained, pcs, turned_pcs, grouped_pcs, pc_codes, sums_out = {}, {}, {}, {}, {}, {}
 
-        def syn(i):
+        def score(i):
             b, r = i // TILES, i % TILES
-            cols = slice(r * P, (r + 1) * P)
-            halves = []
-            for n in range(2):
-                ps = ps_syn.tile([P, 512], F32, name="ps")
-                halves.append(ps)
-                keys = slice(n * 512, (n + 1) * 512)
+            rows = slice(r * P, (r + 1) * P)
+            scores[i] = []
+            for g in range(HALVES):
+                bank = ps_score.tile([P, BANK], F32, name="score")
+                keys = slice(g * BANK, (g + 1) * BANK)
                 nc.tensor.matmul_mx(
-                    out=ps[:],
-                    lhsT=x_codes[b][:, cols].bitcast(FP8X4),
-                    lhsT_scale=x_scales[b][:, cols],
+                    out=bank[:],
+                    lhsT=x_codes[b][:, rows].bitcast(FP8X4),
+                    lhsT_scale=x_scales[b][:, rows],
                     rhs=w_codes[:, keys].bitcast(FP8X4),
                     rhs_scale=w_scales[:, keys],
                     start=True,
                     stop=True,
                 )
-            st[("ps", i)] = halves
+                scores[i].append(bank)
 
         def blend(i):
-            r = i % TILES
-            halves = st.get(("ps", i))
-            logit = work.tile([P, S], F32, name="logit", bufs=3)
-            if i in GPSIMD_MIX:
-                part = work.tile([P, S], F32, name="part")
-                for n in range(2):
-                    keys = slice(n * 512, (n + 1) * 512)
-                    nc.scalar.activation(out=part[:, keys], in_=halves[n][:], func=Act.Copy, scale=mix_f[:, 0:1])
-                nc.gpsimd.tensor_tensor(out=logit[:], in0=part[:], in1=rnd_f[:, r], op=Alu.add)
-                st[("logit", i)] = logit
-                return
-            for n in range(2):
-                keys = slice(n * 512, (n + 1) * 512)
+            logits[i] = work.tile([P, S], F32, name="logit", bufs=3)
+            for g in range(HALVES):
+                keys = slice(g * BANK, (g + 1) * BANK)
                 nc.vector.scalar_tensor_tensor(
-                    out=logit[:, keys],
-                    in0=halves[n][:],
+                    out=logits[i][:, keys],
+                    in0=scores[i][g][:],
                     scalar=mix_f[:, 0:1],
-                    in1=rnd_f[:, r, keys],
+                    in1=rnd_f[:, i % TILES, keys],
                     op0=Alu.mult,
                     op1=Alu.add,
                 )
-            st[("logit", i)] = logit
 
-        def top(i):
-            logit = st.get(("logit", i))
-            nmax = work.tile([P, 1], F32, name="nmax", bufs=4)
-            nc.vector.tensor_reduce(out=nmax[:], in_=logit[:], axis=AX.X, op=Alu.max, negate=True)
-            st[("logit", i)] = (logit, nmax)
+        def maximum(i):
+            maxima[i] = work.tile([P, 1], F32, name="maximum", bufs=4)
+            nc.vector.tensor_reduce(out=maxima[i][:], in_=logits[i][:], axis=AX.X, op=Alu.max, negate=True)
 
         def exponent(i):
-            logit, nmax = st.get(("logit", i))
-            e = work.tile([P, S], F32, name="e", bufs=3)
-            total = work.tile([P, 1], F32, name="total", bufs=4)
-            nc.scalar.activation(out=e[:], in_=logit[:], func=Act.Exp, bias=nmax[:], accum_out=total[:])
-            st[("e", i)] = (e, total)
+            exps[i] = work.tile([P, S], F32, name="exp", bufs=3)
+            totals[i] = work.tile([P, 1], F32, name="total", bufs=4)
+            nc.scalar.activation(
+                out=exps[i][:], in_=logits[i][:], func=Act.Exp, bias=maxima[i][:], accum_out=totals[i][:]
+            )
 
         def invert(i):
-            total = st.get(("e", i))[1]
-            rinv = work.tile([P, 1], F32, name="rinv", bufs=4)
-            nc.vector.reciprocal(out=rinv[:], in_=total[:])
-            st[("rinv", i)] = rinv
+            inverses[i] = work.tile([P, 1], F32, name="inverse", bufs=4)
+            nc.vector.reciprocal(out=inverses[i][:], in_=totals[i][:])
 
         def gain(i):
-            e = st.get(("e", i))[0]
-            if i in VECTOR_TILES:
-                return
-            ec = work.tile([P, S], F32, name="ec", bufs=3)
-            nc.gpsimd.tensor_tensor(out=ec[:], in0=e[:], in1=c_f[:], op=Alu.mult)
-            st[("ec", i)] = ec
+            if i not in VECTOR_TILES:
+                gained[i] = work.tile([P, S], F32, name="gained", bufs=3)
+                nc.gpsimd.tensor_tensor(out=gained[i][:], in0=exps[i][:], in1=c_f[:], op=Alu.mult)
 
         def normalise(i):
-            rinv = st.get(("rinv", i))
-            pc = work.tile([P, S], BF16, name="pc")
+            pcs[i] = work.tile([P, S], BF16, name="pc")
             if i in VECTOR_TILES:
-                e = st.get(("e", i))[0]
-                nc.vector.scalar_tensor_tensor(out=pc[:], in0=e[:], scalar=rinv[:], in1=c_f[:], op0=Alu.mult, op1=Alu.mult)
-            elif i in GPSIMD_NORM:
-                nc.gpsimd.tensor_scalar(out=pc[:], in0=st.get(("ec", i))[:], scalar1=rinv[:], scalar2=1.0, op0=Alu.mult, op1=Alu.mult)
+                nc.vector.scalar_tensor_tensor(
+                    out=pcs[i][:],
+                    in0=exps[i][:],
+                    scalar=inverses[i][:],
+                    in1=c_f[:],
+                    op0=Alu.mult,
+                    op1=Alu.mult,
+                )
             else:
-                nc.scalar.activation(out=pc[:], in_=st.get(("ec", i))[:], func=Act.Copy, scale=rinv[:])
-            st[("pc", i)] = pc
+                nc.scalar.activation(
+                    out=pcs[i][:], in_=gained[i][:], func=Act.Copy, scale=inverses[i][:]
+                )
 
         def turn(i):
-            pc = st.get(("pc", i))
-            words = pc[:].bitcast(F32)
-            tr = ps_tr.tile([P, 2, 2, P], F32, name="tr")
-            for g in range(2):
-                for e in range(2):
-                    first = 256 * g + P * e
-                    nc.tensor.transpose(tr[:, g, e, :], words[:, first : first + P], ident[:])
-            st[("tr", i)] = tr
+            words = pcs[i][:].bitcast(F32)
+            turned_pcs[i] = ps_turn.tile([P, HALVES, 2, P], F32, name="turned")
+            for g in range(HALVES):
+                for h in range(2):
+                    first = g * 2 * P + h * P
+                    nc.tensor.transpose(turned_pcs[i][:, g, h, :], words[:, first : first + P], ident[:])
 
         def turn_out(i):
-            tr = st.get(("tr", i))
-            pg = work.tile([P, 2, P, PACK], BF16, name="pg", bufs=3, align_bytes=64)
-            nc.scalar.copy(out=pg[:].bitcast(F32), in_=tr[:].rearrange("p g e q -> p g q e"))
-            st[("pg", i)] = pg
+            grouped_pcs[i] = work.tile([P, HALVES, P, PACK], BF16, name="p_grouped", bufs=3, align_bytes=64)
+            nc.scalar.copy(
+                out=grouped_pcs[i][:].bitcast(F32),
+                in_=turned_pcs[i][:].rearrange("p g h q -> p g q h"),
+            )
 
         def p_quantize(i):
-            pg = st.get(("pg", i))
-            p_codes = work.tile([P, 2, P], U32, name="p_codes", bufs=4, align_bytes=64)
-            p_scales = work.tile([P, 2, P], U8, name="p_scales", bufs=4, align_bytes=64)
+            p_codes = work.tile([P, HALVES, P], U32, name="p_codes", bufs=4, align_bytes=64)
+            p_scales = work.tile([P, HALVES, P], U8, name="p_scales", bufs=4, align_bytes=64)
             nc.vector.quantize_mx(
                 out=p_codes[:].rearrange("p g q -> p (g q)").bitcast(FP8X4),
                 scales=p_scales[:].rearrange("p g q -> p (g q)"),
-                in_=pg[:].rearrange("p g q t -> p (g q t)"),
+                in_=grouped_pcs[i][:].rearrange("p g q t -> p (g q t)"),
             )
-            st[("p", i)] = (p_codes, p_scales)
+            pc_codes[i] = (p_codes, p_scales)
 
         def product(i):
             b = i // TILES
-            p_codes, p_scales = st.get(("p", i))
-            if i < N_STEPS - 4:
-                acc = ps_acc.tile([P, D], F32, name="acc")
+            p_codes, p_scales = pc_codes[i]
+            if i in SPARE_BANK_TILES:
+                sums_out[i] = ps_prep.tile([P, D], F32, name="prep")
             else:
-                acc = ps_prep.tile([P, D], F32, name="prep")
-            for g in range(2):
+                sums_out[i] = ps_sum.tile([P, D], F32, name="sum")
+            for g in range(HALVES):
                 nc.tensor.matmul_mx(
-                    out=acc[:],
+                    out=sums_out[i][:],
                     lhsT=p_codes[:, g, :].bitcast(FP8X4),
                     lhsT_scale=p_scales[:, g, :],
                     rhs=v_codes[b][:, g, :].bitcast(FP8X4),
                     rhs_scale=v_scales[b][:, g, :],
                     start=(g == 0),
-                    stop=(g == 1),
+                    stop=(g == HALVES - 1),
                 )
-            st[("acc", i)] = acc
 
         def store(i):
             b, r = i // TILES, i % TILES
-            o = work.tile([P, D], F32, name="o", bufs=4)
-            nc.scalar.copy(out=o[:], in_=st.get(("acc", i))[:])
-            nc.sync.dma_start(out=out_v[b, :, r // PACK, r % PACK], in_=o[:])
+            rows_out = work.tile([P, D], F32, name="rows_out", bufs=4)
+            nc.scalar.copy(out=rows_out[:], in_=sums_out[i][:])
+            nc.sync.dma_start(out=out_rows[b, :, r // PACK, r % PACK], in_=rows_out[:])
 
-        plan = {}
-        late = {}
-        middle = {}
-        early = {}
-        second = {}
-        extra = {}
+        before, head, opening, middle, closing, rnd_plan = {}, {}, {}, {}, {}, {}
 
-        def put(step, fn, *args):
-            plan.setdefault(step, []).append((fn, args))
+        def put(plan, step, stage, *args):
+            plan.setdefault(step, []).append((stage, args))
+
+        def run(plan, step):
+            for stage, args in plan.get(step, []):
+                stage(*args)
 
         for b in range(B):
             if b > 0:
                 for k in range(4):
-                    put(8 * b - 2 + k, x_third, b, k)
-                    late.setdefault(8 * b - 4 + k, []).append((x_turn, (b, k)))
-                    second.setdefault(8 * b - 3 + k, []).append((x_second, (b, k)))
-                    put(8 * b - 4 + k, x_first, b, k)
-            put(8 * b + 3, v_quantize, b, 0)
-            put(8 * b + 4, v_quantize, b, 1)
-            for i in range(8):
-                step = 8 * b + i // 2 if b > 0 else 2 + i // 4
-                if b > 0:
-                    late.setdefault(step - 1, []).append((v_product, (b, i // 4, i % 4)))
-                elif i % 4 < 2:
-                    early.setdefault(step, []).append((v_product, (b, i // 4, i % 4)))
-                else:
-                    middle.setdefault(step, []).append((v_product, (b, i // 4, i % 4)))
-                middle.setdefault(step, []).append((v_gain, (b, i // 4, i % 4)))
-        for i in range(3, TILES):
-            extra.setdefault(max(2, i - 2), []).append((rnd_scale, (i,)))
+                    put(before, 8 * b - 3 + k, x_copy_out, b, k)
+                    put(head, 8 * b - 2 + k, x_quantize, b, k)
+                    put(head, 8 * b - 4 + k, x_scaled, b, k)
+                    put(closing, 8 * b - 4 + k, x_turn, b, k)
+            put(head, 8 * b + 3, v_quantize, b, 0)
+            put(head, 8 * b + 4, v_quantize, b, 1)
+            for h in range(HALVES):
+                for n in range(4):
+                    if b > 0:
+                        step = 8 * b + 2 * h + n // 2
+                        put(closing, step - 1, v_product, b, h, n)
+                    else:
+                        step = 2 + h
+                        put(opening if n < 2 else middle, step, v_product, b, h, n)
+                    put(middle, step, v_gain, b, h, n)
+        for r in range(3, TILES):
+            put(rnd_plan, max(2, r - 3), rnd_scale, r)
 
         with tc.manual_schedule():
-            w_grouped = []
-            for n in range(2):
-                w_grouped.append(keep.tile([P, 512, PACK], BF16, name="w_grouped%d" % n, align_bytes=64))
-            wv_grouped = keep.tile([P, D, PACK], BF16, name="wv_grouped", align_bytes=64)
-            w_copy(0)
-            x_widen(0, 0)
+            w_group(0)
+            x_plain(0, 0)
             x_turn(0, 0)
-            weight_quantize(w_grouped[0], w_codes, w_scales, slice(0, 512))
-            nc.vector.tensor_copy(out=mix_f[:], in_=mix_b[:])
-            nc.vector.tensor_copy(out=u_f[:], in_=u_b[:])
-            w_copy(1)
-            x_widen(0, 1)
+            w_quantize(0)
+            nc.vector.tensor_copy(out=mix_f[:], in_=mix_raw[:])
+            nc.vector.tensor_copy(out=u_f[:], in_=u_raw[:])
+            w_group(1)
+            x_plain(0, 1)
             x_turn(0, 1)
-            x_scale_out(0, 0)
+            x_scaled_late(0, 0)
             rnd_scale(0)
-            weight_quantize(w_grouped[1], w_codes, w_scales, slice(512, 1024))
-            x_scale_out(0, 1)
-            x_third(0, 0)
-            syn(0)
-            x_third(0, 1)
+            w_quantize(1)
+            x_scaled_late(0, 1)
+            x_quantize(0, 0)
+            score(0)
+            x_quantize(0, 1)
             rnd_scale(1)
             c_spread()
-            weight_copy(wv_raw, D, slice(0, D), wv_grouped, False)
-            nc.vector.tensor_copy(out=xs[:, D : 2 * D], in_=xs[:, 0:D])
+            wv_group()
+            nc.vector.tensor_copy(out=scale_row[:, D : 2 * D], in_=scale_row[:, 0:D])
             blend(0)
-            syn(1)
-            x_first(0, 2)
+            score(1)
+            x_scaled(0, 2)
             x_turn(0, 2)
-            top(0)
-            x_first(0, 3)
+            maximum(0)
+            x_scaled(0, 3)
             x_turn(0, 3)
-            x_second(0, 2)
+            x_copy_out(0, 2)
             blend(1)
-            syn(2)
+            score(2)
             rnd_scale(2)
-            x_second(0, 3)
+            x_copy_out(0, 3)
             exponent(0)
             gain(0)
-            top(1)
-            x_third(0, 2)
-            x_third(0, 3)
+            maximum(1)
+            x_quantize(0, 2)
+            x_quantize(0, 3)
 
-            for s in range(2, N_STEPS + 5):
-                if s <= N_STEPS:
+            for s in range(2, N_TILES + 4):
+                if s <= N_TILES:
                     exponent(s - 1)
                     gain(s - 1)
-                for fn, args in second.get(s, []):
-                    fn(*args)
-                if 0 <= s - 3 < N_STEPS:
+                run(before, s)
+                if 0 <= s - 3 < N_TILES:
                     turn_out(s - 3)
-                if 0 <= s - 4 < N_STEPS:
+                if 0 <= s - 4 < N_TILES:
                     p_quantize(s - 4)
-                for fn, args in plan.get(s, []):
-                    fn(*args)
+                run(head, s)
                 if s == 2:
-                    weight_quantize(wv_grouped, wv_codes, wv_scales, slice(0, D))
+                    wv_quantize()
                     invert(0)
-                if 0 <= s - 2 < N_STEPS:
+                if 0 <= s - 2 < N_TILES:
                     normalise(s - 2)
-                for fn, args in extra.get(s, []):
-                    fn(*args)
-                if 0 <= s - 4 < N_STEPS:
+                run(rnd_plan, s)
+                if 0 <= s - 4 < N_TILES:
                     product(s - 4)
-                for fn, args in early.get(s, []):
-                    fn(*args)
-                if s < N_STEPS:
+                run(opening, s)
+                if s < N_TILES:
                     blend(s)
-                if s + 1 < N_STEPS:
-                    syn(s + 1)
-                for fn, args in middle.get(s, []):
-                    fn(*args)
-                if s <= N_STEPS:
+                if s + 1 < N_TILES:
+                    score(s + 1)
+                run(middle, s)
+                if s <= N_TILES:
                     invert(s - 1)
-                if s < N_STEPS:
-                    top(s)
-                if 0 <= s - 2 < N_STEPS:
+                if s < N_TILES:
+                    maximum(s)
+                if 0 <= s - 2 < N_TILES:
                     turn(s - 2)
-                if 0 <= s - 4 < N_STEPS:
+                if 0 <= s - 4 < N_TILES:
                     store(s - 4)
-                for fn, args in late.get(s, []):
-                    fn(*args)
+                run(closing, s)

from contextlib import ExitStack

import concourse.mybir as mybir
from concourse.masks import make_identity

B, S, D = 4, 1024, 512
P = 128
PACK = 4
HALF = P * PACK
HALVES = S // HALF
TILES = S // P
N_TILES = B * TILES
BANK = 512

F32 = mybir.dt.float32
BF16 = mybir.dt.bfloat16
U32 = mybir.dt.uint32
U8 = mybir.dt.uint8
FP8 = mybir.dt.float8_e4m3fn
FP8X4 = mybir.dt.float8_e4m3fn_x4
Alu = mybir.AluOpType
Act = mybir.ActivationFunctionType
AX = mybir.AxisListType

FLOPS = 2 * B * S * D * S + 2 * B * S * D * D + 2 * B * S * S * D

VECTOR_TILES = (N_TILES - 3, N_TILES - 2, N_TILES - 1)

SPARE_BANK_TILES = range(N_TILES - 4, N_TILES)


def tile_mixturedenserandomsynthesizer_t_kernel(tc, x_bytes, x_scale, w, rnd, mix, wv, c, u, out):
    nc = tc.nc
    with ExitStack() as ctx:
        keep = ctx.enter_context(tc.tile_pool(name="keep", bufs=1))
        work = ctx.enter_context(tc.tile_pool(name="work", bufs=2))
        ps_score = ctx.enter_context(tc.psum_pool(name="ps_score", bufs=3))
        ps_turn = ctx.enter_context(tc.psum_pool(name="ps_turn", bufs=1))
        ps_sum = ctx.enter_context(tc.psum_pool(name="ps_sum", bufs=1))
        ps_prep = ctx.enter_context(tc.psum_pool(name="ps_prep", bufs=3))

        x_scale_flat = x_scale.rearrange("a b k -> (a b k)")
        scale_4 = keep.tile([P, PACK], F32, name="scale_4")
        nc.scalar.dma_start(out=scale_4[:], in_=x_scale_flat.rearrange("(p t) -> p t", t=PACK))
        mix_raw = keep.tile([P, 2], BF16, name="mix_raw")
        nc.scalar.dma_start(out=mix_raw[:], in_=mix.partition_broadcast(P))
        u_raw = keep.tile([P, HALVES, PACK], BF16, name="u_raw")
        nc.scalar.dma_start(out=u_raw[:], in_=u.rearrange("(h p t) -> p h t", p=P, t=PACK))
        c_row = keep.tile([P, S], BF16, name="c_row")
        nc.gpsimd.memset(c_row[:], 0.0)
        ones = keep.tile([P, P], BF16, name="ones")
        nc.gpsimd.memset(ones[:], 1.0)
        nc.scalar.dma_start(out=c_row[0:1, :], in_=c.rearrange("(o k) -> o k", o=1))

        x_rows = x_bytes.rearrange("b (h m t) k -> b m h t k", m=P, t=PACK)
        x_raw = []
        for b in range(B):
            x_raw.append(keep.tile([P, HALVES, PACK, D], U8, name="x_raw%d" % b, align_bytes=64))
        rnd_rows = rnd.rearrange("(h m t) k -> m h t k", m=P, t=PACK)
        rnd_raw = keep.tile([P, TILES, S], BF16, name="rnd_raw")
        w_rows = w.rearrange("(p j) n -> p j n", j=PACK)
        w_raw = keep.tile([P, PACK, S], BF16, name="w_raw")
        wv_raw = keep.tile([P, PACK, D], BF16, name="wv_raw")
        scale_row = keep.tile([P, 2 * D], F32, name="scale_row")

        nc.sync.dma_start(out=w_raw[:, :, 0:BANK], in_=w_rows[:, :, 0:BANK])
        nc.sync.dma_start(out=x_raw[0][:, 0], in_=x_rows[0, :, 0])
        nc.sync.dma_start(out=w_raw[:, :, BANK:S], in_=w_rows[:, :, BANK:S])
        nc.sync.dma_start(out=rnd_raw[:, 0:2], in_=rnd_rows[:, 0, 0:2])
        nc.sync.dma_start(out=x_raw[0][:, 1], in_=x_rows[0, :, 1])
        nc.sync.dma_start(out=scale_row[:, 0:D], in_=x_scale_flat.partition_broadcast(P))
        nc.sync.dma_start(out=wv_raw[:], in_=wv.rearrange("(p j) n -> p j n", j=PACK))
        nc.sync.dma_start(out=rnd_raw[:, 2:4], in_=rnd_rows[:, 0, 2:4])
        nc.sync.dma_start(out=rnd_raw[:, 4:8], in_=rnd_rows[:, 1])
        for b in range(1, B):
            nc.sync.dma_start(out=x_raw[b][:], in_=x_rows[b])

        ident = keep.tile([P, P], F32, name="ident")
        make_identity(nc, ident[:])
        warm = keep.tile([P, 1], F32, name="warm")
        nc.vector.memset(warm[:], 0.0)
        nc.scalar.activation(out=warm[:], in_=warm[:], func=Act.Exp)
        mix_f = keep.tile([P, 2], F32, name="mix_f")
        u_f = keep.tile([P, HALVES, PACK], F32, name="u_f")
        c_f = keep.tile([P, S], F32, name="c_f")
        rnd_f = keep.tile([P, TILES, S], F32, name="rnd_f")

        w_grouped = []
        for g in range(HALVES):
            w_grouped.append(keep.tile([P, BANK, PACK], BF16, name="w_grouped%d" % g, align_bytes=64))
        wv_grouped = keep.tile([P, D, PACK], BF16, name="wv_grouped", align_bytes=64)
        w_codes = keep.tile([P, S], U32, name="w_codes", align_bytes=64)
        w_scales = keep.tile([P, S], U8, name="w_scales", align_bytes=64)
        wv_codes = keep.tile([P, D], U32, name="wv_codes", align_bytes=64)
        wv_scales = keep.tile([P, D], U8, name="wv_scales", align_bytes=64)
        x_codes, x_scales, v_codes, v_scales = [], [], [], []
        for b in range(B):
            x_codes.append(keep.tile([P, S], U32, name="x_codes%d" % b, align_bytes=64))
            x_scales.append(keep.tile([P, S], U8, name="x_scales%d" % b, align_bytes=64))
            v_codes.append(keep.tile([P, HALVES, D], U32, name="v_codes%d" % b, align_bytes=64))
            v_scales.append(keep.tile([P, HALVES, D], U8, name="v_scales%d" % b, align_bytes=64))

        out_rows = out.rearrange("b (h m t) d -> b m h t d", m=P, t=PACK)

        def key_columns(ap):
            return ap.rearrange("p (m h e) -> p h m e", h=2, e=2)

        def columns_split(ap):
            return ap.rearrange("p (h m e) -> p h m e", h=2, e=2)

        def w_group(g):
            src = w_raw[:, :, g * BANK : (g + 1) * BANK].rearrange("p j (m h e) -> p h m e j", h=2, e=2)
            dst = w_grouped[g][:].rearrange("p (h m e) j -> p h m e j", h=2, e=2)
            for h in range(2):
                nc.vector.tensor_copy(out=dst[:, h], in_=src[:, h])

        def w_quantize(g):
            cols = slice(g * BANK, (g + 1) * BANK)
            nc.vector.quantize_mx(
                out=w_codes[:, cols].bitcast(FP8X4),
                scales=w_scales[:, cols],
                in_=w_grouped[g][:].rearrange("p n j -> p (n j)"),
            )

        def wv_group():
            nc.scalar.copy(out=wv_grouped[:], in_=wv_raw[:].rearrange("p j n -> p n j"))

        def wv_quantize():
            nc.vector.quantize_mx(
                out=wv_codes[:].bitcast(FP8X4),
                scales=wv_scales[:],
                in_=wv_grouped[:].rearrange("p n j -> p (n j)"),
            )

        def rnd_scale(r):
            for g in range(HALVES):
                cols = slice(g * BANK, (g + 1) * BANK)
                nc.scalar.activation(
                    out=columns_split(rnd_f[:, r, cols]),
                    in_=key_columns(rnd_raw[:, r, cols]),
                    func=Act.Copy,
                    scale=mix_f[:, 1:2],
                )

        def c_spread():
            for g in range(HALVES):
                cols = slice(g * BANK, (g + 1) * BANK)
                spread = ps_prep.tile([P, BANK], F32, name="prep")
                nc.tensor.matmul(spread[:], lhsT=ones[:], rhs=c_row[:, cols], start=True, stop=True)
                nc.scalar.copy(out=columns_split(c_f[:, cols]), in_=key_columns(spread[:]))

        x_wide, x_turned, x_grouped = {}, {}, {}

        def x_codes_of(b, k):
            h, t = k // 2, 2 * (k % 2)
            return x_raw[b][:, h, t : t + 2, :].rearrange("p t k -> p (t k)").bitcast(FP8)

        def x_scaled(b, k):
            wide = work.tile([P, 2 * D], BF16, name="wide")
            nc.vector.tensor_tensor(out=wide[:], in0=x_codes_of(b, k), in1=scale_row[:], op=Alu.mult)
            x_wide[(b, k)] = wide

        def x_plain(b, k):
            wide = work.tile([P, 2 * D], BF16, name="wide")
            nc.scalar.copy(out=wide[:], in_=x_codes_of(b, k))
            x_wide[(b, k)] = wide

        def x_turn(b, k):
            words = x_wide.get((b, k))[:].bitcast(F32)
            turned = ps_prep.tile([P, 2, 2, P], F32, name="prep")
            for j in range(2):
                for e in range(2):
                    nc.tensor.transpose(turned[:, j, e, :], words[:, 256 * j + e : 256 * (j + 1) : 2], ident[:])
            x_turned[(b, k)] = turned

        def x_copy_out(b, k):
            grouped = work.tile([P, 2, P, PACK], BF16, name="x_grouped", align_bytes=64)
            nc.scalar.copy(
                out=grouped[:].bitcast(F32), in_=x_turned.get((b, k))[:].rearrange("p j e q -> p j q e")
            )
            x_grouped[(b, k)] = grouped

        def x_scaled_late(b, k):
            turned = x_turned.get((b, k))
            grouped = work.tile([P, 2, P, PACK], BF16, name="x_grouped", align_bytes=64)
            for j in range(2):
                nc.vector.tensor_tensor(
                    out=grouped[:, j].rearrange("p q (h e) -> p q h e", e=2),
                    in0=turned[:, j]
                    .rearrange("p h q -> p (h q)")
                    .bitcast(BF16)
                    .rearrange("p (h q e) -> p q h e", h=2, e=2),
                    in1=scale_4[:].rearrange("p (o h e) -> p o h e", o=1, e=2).to_broadcast([P, P, 2, 2]),
                    op=Alu.mult,
                )
            x_grouped[(b, k)] = grouped

        def x_quantize(b, k):
            cols = slice(2 * P * k, 2 * P * (k + 1))
            nc.vector.quantize_mx(
                out=x_codes[b][:, cols].bitcast(FP8X4),
                scales=x_scales[b][:, cols],
                in_=x_grouped.get((b, k))[:].rearrange("p j q t -> p (j q t)"),
            )

        v_sums, v_grouped = {}, {}

        def v_product(b, h, n):
            sums = ps_prep.tile([P, PACK, P], F32, name="prep")
            d_cols = slice(n * P, (n + 1) * P)
            for t in range(PACK):
                rows = slice((h * PACK + t) * P, (h * PACK + t + 1) * P)
                nc.tensor.matmul_mx(
                    out=sums[:, t, :],
                    lhsT=x_codes[b][:, rows].bitcast(FP8X4),
                    lhsT_scale=x_scales[b][:, rows],
                    rhs=wv_codes[:, d_cols].bitcast(FP8X4),
                    rhs_scale=wv_scales[:, d_cols],
                    start=True,
                    stop=True,
                )
            v_sums[(b, h, n)] = sums

        def v_gain(b, h, n):
            if n == 0:
                v_grouped[(b, h)] = work.tile([P, D, PACK], BF16, name="v_grouped", align_bytes=64)
            nc.vector.tensor_tensor(
                out=v_grouped.get((b, h))[:, n * P : (n + 1) * P, :],
                in0=v_sums.get((b, h, n))[:].rearrange("p t d -> p d t"),
                in1=u_f[:, h : h + 1, :].to_broadcast([P, P, PACK]),
                op=Alu.mult,
            )

        def v_quantize(b, h):
            nc.vector.quantize_mx(
                out=v_codes[b][:, h, :].bitcast(FP8X4),
                scales=v_scales[b][:, h, :],
                in_=v_grouped.get((b, h))[:].rearrange("p d t -> p (d t)"),
            )

        scores, logits, maxima, exps, totals, inverses = {}, {}, {}, {}, {}, {}
        gained, pcs, turned_pcs, grouped_pcs, pc_codes, sums_out = {}, {}, {}, {}, {}, {}

        def score(i):
            b, r = i // TILES, i % TILES
            rows = slice(r * P, (r + 1) * P)
            scores[i] = []
            for g in range(HALVES):
                bank = ps_score.tile([P, BANK], F32, name="score")
                keys = slice(g * BANK, (g + 1) * BANK)
                nc.tensor.matmul_mx(
                    out=bank[:],
                    lhsT=x_codes[b][:, rows].bitcast(FP8X4),
                    lhsT_scale=x_scales[b][:, rows],
                    rhs=w_codes[:, keys].bitcast(FP8X4),
                    rhs_scale=w_scales[:, keys],
                    start=True,
                    stop=True,
                )
                scores[i].append(bank)

        def blend(i):
            logits[i] = work.tile([P, S], F32, name="logit", bufs=3)
            for g in range(HALVES):
                keys = slice(g * BANK, (g + 1) * BANK)
                nc.vector.scalar_tensor_tensor(
                    out=logits[i][:, keys],
                    in0=scores[i][g][:],
                    scalar=mix_f[:, 0:1],
                    in1=rnd_f[:, i % TILES, keys],
                    op0=Alu.mult,
                    op1=Alu.add,
                )

        def maximum(i):
            maxima[i] = work.tile([P, 1], F32, name="maximum", bufs=4)
            nc.vector.tensor_reduce(out=maxima[i][:], in_=logits[i][:], axis=AX.X, op=Alu.max, negate=True)

        def exponent(i):
            exps[i] = work.tile([P, S], F32, name="exp", bufs=3)
            totals[i] = work.tile([P, 1], F32, name="total", bufs=4)
            nc.scalar.activation(
                out=exps[i][:], in_=logits[i][:], func=Act.Exp, bias=maxima[i][:], accum_out=totals[i][:]
            )

        def invert(i):
            inverses[i] = work.tile([P, 1], F32, name="inverse", bufs=4)
            nc.vector.reciprocal(out=inverses[i][:], in_=totals[i][:])

        def gain(i):
            if i not in VECTOR_TILES:
                gained[i] = work.tile([P, S], F32, name="gained", bufs=3)
                nc.gpsimd.tensor_tensor(out=gained[i][:], in0=exps[i][:], in1=c_f[:], op=Alu.mult)

        def normalise(i):
            pcs[i] = work.tile([P, S], BF16, name="pc")
            if i in VECTOR_TILES:
                nc.vector.scalar_tensor_tensor(
                    out=pcs[i][:],
                    in0=exps[i][:],
                    scalar=inverses[i][:],
                    in1=c_f[:],
                    op0=Alu.mult,
                    op1=Alu.mult,
                )
            else:
                nc.scalar.activation(
                    out=pcs[i][:], in_=gained[i][:], func=Act.Copy, scale=inverses[i][:]
                )

        def turn(i):
            words = pcs[i][:].bitcast(F32)
            turned_pcs[i] = ps_turn.tile([P, HALVES, 2, P], F32, name="turned")
            for g in range(HALVES):
                for h in range(2):
                    first = g * 2 * P + h * P
                    nc.tensor.transpose(turned_pcs[i][:, g, h, :], words[:, first : first + P], ident[:])

        def turn_out(i):
            grouped_pcs[i] = work.tile([P, HALVES, P, PACK], BF16, name="p_grouped", bufs=3, align_bytes=64)
            nc.scalar.copy(
                out=grouped_pcs[i][:].bitcast(F32),
                in_=turned_pcs[i][:].rearrange("p g h q -> p g q h"),
            )

        def p_quantize(i):
            p_codes = work.tile([P, HALVES, P], U32, name="p_codes", bufs=4, align_bytes=64)
            p_scales = work.tile([P, HALVES, P], U8, name="p_scales", bufs=4, align_bytes=64)
            nc.vector.quantize_mx(
                out=p_codes[:].rearrange("p g q -> p (g q)").bitcast(FP8X4),
                scales=p_scales[:].rearrange("p g q -> p (g q)"),
                in_=grouped_pcs[i][:].rearrange("p g q t -> p (g q t)"),
            )
            pc_codes[i] = (p_codes, p_scales)

        def product(i):
            b = i // TILES
            p_codes, p_scales = pc_codes[i]
            if i in SPARE_BANK_TILES:
                sums_out[i] = ps_prep.tile([P, D], F32, name="prep")
            else:
                sums_out[i] = ps_sum.tile([P, D], F32, name="sum")
            for g in range(HALVES):
                nc.tensor.matmul_mx(
                    out=sums_out[i][:],
                    lhsT=p_codes[:, g, :].bitcast(FP8X4),
                    lhsT_scale=p_scales[:, g, :],
                    rhs=v_codes[b][:, g, :].bitcast(FP8X4),
                    rhs_scale=v_scales[b][:, g, :],
                    start=(g == 0),
                    stop=(g == HALVES - 1),
                )

        def store(i):
            b, r = i // TILES, i % TILES
            rows_out = work.tile([P, D], F32, name="rows_out", bufs=4)
            nc.scalar.copy(out=rows_out[:], in_=sums_out[i][:])
            nc.sync.dma_start(out=out_rows[b, :, r // PACK, r % PACK], in_=rows_out[:])

        before, head, opening, middle, closing, rnd_plan = {}, {}, {}, {}, {}, {}

        def put(plan, step, stage, *args):
            plan.setdefault(step, []).append((stage, args))

        def run(plan, step):
            for stage, args in plan.get(step, []):
                stage(*args)

        for b in range(B):
            if b > 0:
                for k in range(4):
                    put(before, 8 * b - 3 + k, x_copy_out, b, k)
                    put(head, 8 * b - 2 + k, x_quantize, b, k)
                    put(head, 8 * b - 4 + k, x_scaled, b, k)
                    put(closing, 8 * b - 4 + k, x_turn, b, k)
            put(head, 8 * b + 3, v_quantize, b, 0)
            put(head, 8 * b + 4, v_quantize, b, 1)
            for h in range(HALVES):
                for n in range(4):
                    if b > 0:
                        step = 8 * b + 2 * h + n // 2
                        put(closing, step - 1, v_product, b, h, n)
                    else:
                        step = 2 + h
                        put(opening if n < 2 else middle, step, v_product, b, h, n)
                    put(middle, step, v_gain, b, h, n)
        for r in range(3, TILES):
            put(rnd_plan, max(2, r - 3), rnd_scale, r)

        with tc.manual_schedule():
            w_group(0)
            x_plain(0, 0)
            x_turn(0, 0)
            w_quantize(0)
            nc.vector.tensor_copy(out=mix_f[:], in_=mix_raw[:])
            nc.vector.tensor_copy(out=u_f[:], in_=u_raw[:])
            w_group(1)
            x_plain(0, 1)
            x_turn(0, 1)
            x_scaled_late(0, 0)
            rnd_scale(0)
            w_quantize(1)
            x_scaled_late(0, 1)
            x_quantize(0, 0)
            score(0)
            x_quantize(0, 1)
            rnd_scale(1)
            c_spread()
            wv_group()
            nc.vector.tensor_copy(out=scale_row[:, D : 2 * D], in_=scale_row[:, 0:D])
            blend(0)
            score(1)
            x_scaled(0, 2)
            x_turn(0, 2)
            maximum(0)
            x_scaled(0, 3)
            x_turn(0, 3)
            x_copy_out(0, 2)
            blend(1)
            score(2)
            rnd_scale(2)
            x_copy_out(0, 3)
            exponent(0)
            gain(0)
            maximum(1)
            x_quantize(0, 2)
            x_quantize(0, 3)

            for s in range(2, N_TILES + 4):
                if s <= N_TILES:
                    exponent(s - 1)
                    gain(s - 1)
                run(before, s)
                if 0 <= s - 3 < N_TILES:
                    turn_out(s - 3)
                if 0 <= s - 4 < N_TILES:
                    p_quantize(s - 4)
                run(head, s)
                if s == 2:
                    wv_quantize()
                    invert(0)
                if 0 <= s - 2 < N_TILES:
                    normalise(s - 2)
                run(rnd_plan, s)
                if 0 <= s - 4 < N_TILES:
                    product(s - 4)
                run(opening, s)
                if s < N_TILES:
                    blend(s)
                if s + 1 < N_TILES:
                    score(s + 1)
                run(middle, s)
                if s <= N_TILES:
                    invert(s - 1)
                if s < N_TILES:
                    maximum(s)
                if 0 <= s - 2 < N_TILES:
                    turn(s - 2)
                if 0 <= s - 4 < N_TILES:
                    store(s - 4)
                run(closing, s)
